import numpy as np, ml_dtypes
CORES = [36,164,52,180,100,228,116,244]
N = 8
BF = ml_dtypes.bfloat16
def gentries(a):
    return np.ascontiguousarray(a.reshape(8, 16, -1).transpose(0, 2, 1)).reshape(8, -1)
def gtable(e):
    e = np.asarray(e); return np.ascontiguousarray(e.reshape(8, -1, 16).transpose(0, 2, 1)).reshape(128, -1).astype(np.int32)
DR, NZ, Z, R = 1, 2, 2304, 4
ND, DD, C = N * DR, N * DR - 2, 2 * Z // R
def disks(x):
    return np.ascontiguousarray(x.astype(np.float32).astype(np.int32).reshape(N, 128, DR, NZ, Z).transpose(0, 2, 3, 1, 4)).reshape(ND, NZ, 128, Z)
def turns(pi):
    return np.ascontiguousarray(np.stack([gentries(a) for a in pi]).reshape(N, 8, DR, NZ, Z).transpose(0, 2, 3, 1, 4)).reshape(ND, NZ, 8, Z)
def follow(pa, pb):
    inv = np.zeros(Z, np.int64); inv[pb] = np.arange(Z)
    return inv, pa[inv]
def solve(w, p, a, b, ze):
    ps = w[DD].copy(); qs = w[DD + 1].copy()
    for i in range(DD):
        if i != a and i != b: ps -= w[i]; qs -= w[i][:, p[i]]
    ps = np.ascontiguousarray(ps.T) & 255; qs = np.ascontiguousarray(qs.T) & 255
    inv, nx = follow(p[a], p[b]); d = ps - qs[inv]; live = (ze == 0)[:, None]; xa = np.zeros((Z, 16), np.int32)
    for s in range(128): xa = np.where(live, d + xa[nx], 0) & 255
    return xa, (ps - xa) & 255, qs
def some_bytes(rng, *shape):
    return rng.integers(0, 256, shape, dtype=np.uint8).astype(np.int32)
def some_turns(rng):
    return rng.permuted(np.tile(np.arange(Z), (DD, NZ, 8, 1)), axis=-1)
def some_pairs(rng):
    o = rng.permutation(DD); return np.array([[o[g % DD], o[(g + rng.integers(1, DD)) % DD]] for g in range(8)])
def marks(rng, nx, gaps, first):
    m = np.zeros(Z, bool); n = nx.tolist(); seen = [False] * Z; u = 0
    for s in first + rng.permutation(Z).tolist():
        left = 0
        while not seen[s]:
            seen[s] = True
            if left == 0: m[s] = True; left = gaps[u]; u += 1
            left -= 1; s = n[s]
    return m
def write(rng, v, p, lo, far=False, first=None):
    ze = np.zeros((NZ, 8, Z), bool); qs = np.zeros((NZ, 128, Z), np.int32)
    for z in range(NZ):
        for g in range(8):
            a, b = lo[g]; k = slice(16 * g, 16 * g + 16)
            gaps = np.where(rng.random(Z) < (1 if far else 0.25), 128, rng.integers(1, 129, Z)).tolist()
            ze[z, g] = marks(rng, follow(p[a, z, g], p[b, z, g])[1], gaps, [] if first is None else first[g])
            v[a, z, k] *= ~ze[z, g]
            for i in range(DD): qs[z, k] += v[i, z, k][:, p[i, z, g]]
    ps = np.add.reduce(v, axis=0)
    for g in range(8):
        for i in lo[g]: v[i, :, 16 * g:16 * g + 16] = some_bytes(rng, NZ, 16, Z)
    w = np.concatenate([v, ps[None] & 255, qs[None] & 255]); t = np.concatenate([p, np.tile(np.arange(Z), (2, NZ, 8, 1))])
    t = t.reshape(N, DR, NZ, 8, Z).transpose(0, 3, 1, 2, 4).reshape(N, 8, -1)
    return {"x": np.ascontiguousarray(w.reshape(N, DR, NZ, 128, Z).transpose(0, 3, 1, 2, 4)).reshape(N, 128, -1).astype(np.float32).astype(BF),
            "pi": np.stack([gtable(e) for e in t]), "lost": np.stack([np.repeat(lo, 16, axis=0).astype(np.int32)] * N), "zero": np.stack([gtable(ze[q // R]) for q in range(N)])}
def setup_inputs(rng):
    return write(rng, some_bytes(rng, DD, NZ, 128, Z), some_turns(rng), some_pairs(rng))
def setup_inputs_long(rng):
    p = some_turns(rng); lo = some_pairs(rng)
    for z in range(NZ):
        for g in range(8):
            o = np.arange(Z) if g == 0 else np.arange(Z)[::-1] if g == 1 else rng.permutation(Z)
            c = np.zeros(Z, np.int64); c[o] = np.roll(o, -1); a, b = lo[g]; p[a, z, g] = c[p[b, z, g]]
    return write(rng, some_bytes(rng, DD, NZ, 128, Z), p, lo, True, [[0], [Z - 1]] + [[]] * 6)
def setup_inputs_short(rng):
    p = some_turns(rng); lo = some_pairs(rng); h = rng.permutation(8)
    for z in range(NZ):
        for u in range(6):
            g = h[u]; a, b = lo[g]; o = rng.permutation(Z); c = np.arange(Z)
            if u == 1: c[o[0::2]] = o[1::2]; c[o[1::2]] = o[0::2]
            if u == 2:
                i = 0
                while i < Z:
                    n = int(rng.integers(1, 6)); k = o[i:i + n]; c[k] = np.roll(k, -1); i += n
            if u < 3: p[a, z, g] = c[p[b, z, g]]
            if u == 3:
                for i in range(DD):
                    if i != a and i != b: p[i, z, g] = np.arange(Z)
            if u == 4: p[b, z, g] = np.arange(Z)
            if u == 5: p[a, z, g] = np.arange(Z)
    return write(rng, some_bytes(rng, DD, NZ, 128, Z), p, lo, True)
def setup_inputs_pair(rng):
    lo = np.array([[0, DD - 1] if e else [DD - 1, 0] for e in rng.permutation(8) < 4])
    return write(rng, some_bytes(rng, DD, NZ, 128, Z), some_turns(rng), lo)
def setup_inputs_spread(rng):
    v = some_bytes(rng, DD, NZ, 128, Z) & rng.choice(np.array([0, 1, 3, 15, 63, 128, 255], np.int32), (DD, NZ, 1, Z))
    v[rng.random(v.shape, dtype=np.float32) < 0.2] = 255
    return write(rng, v, some_turns(rng), some_pairs(rng))
def check_inputs(d):
    bad = []; x = d["x"].astype(np.float32); p = turns(d["pi"]); lo = d["lost"]; ze = d["zero"]
    if not ((x >= 0) & (x <= 255) & (x == np.floor(x))).all(): bad.append("bytes")
    if not (np.sort(p, axis=-1) == np.arange(Z)).all(): bad.append("permutations")
    if not (p[DD:] == np.arange(Z)).all(): bad.append("identity")
    if not ((lo >= 0) & (lo < DD)).all() or not (lo[:, :, 0] != lo[:, :, 1]).all() or not (lo == np.repeat(lo[0, ::16], 16, axis=0)).all(): bad.append("lost")
    if not ((ze == 0) | (ze == 1)).all() or not all((ze[q] == ze[q - q % R]).all() for q in range(N)): bad.append("zero")
    if bad: return bad
    v = disks(d["x"])
    for z in range(NZ):
        e = gentries(ze[z * R])
        for g in range(8):
            a, b = int(lo[0, 16 * g, 0]), int(lo[0, 16 * g, 1]); nx = follow(p[a, z, g], p[b, z, g])[1]; m = e[g][nx] == 1; first = m
            for s in range(127): m = first | m[nx]
            if not m.all(): bad.append("chains")
            xa, xb, qs = solve(v[:, z, 16 * g:16 * g + 16], p[:, z, g], a, b, e[g])
            if not (((xa[p[a, z, g]] + xb[p[b, z, g]]) & 255) == qs).all(): bad.append("sums")
    return sorted(set(bad))
def reference(x, pi, lost, zero):
    v = disks(x); p = turns(pi); y = np.zeros((N, 128, C), np.float32)
    for z in range(NZ):
        e = gentries(zero[z * R])
        for g in range(8):
            xa, xb, qs = solve(v[:, z, 16 * g:16 * g + 16], p[:, z, g], int(lost[0, 16 * g, 0]), int(lost[0, 16 * g, 1]), e[g])
            both = np.concatenate([xa, xb]).T
            for s in range(R): y[z * R + s, 16 * g:16 * g + 16] = both[:, s * C:(s + 1) * C]
    return {"y": y.astype(BF)}

@@ -1,0 +1,656 @@
+from concourse.bass import DstId, RemoteDMATransfer
+from concourse.mybir import AluOpType as Op, ActivationFunctionType as Act
+
+N, R, Z, DD = 8, 4, 2304, 6
+HALF, QUART, PIECE, CH = Z // 2, Z // 4, Z // 8, Z // 6
+LC = Z // 16
+OFFSET = 49152.0
+MAGIC = 3221225472.0
+
+
+def sb(cols, dtype):
+    return ("sbuf", [128, cols], dtype)
+
+
+SCRATCH = {
+    "PS": ("dram", [N * 128, 36], "int32"), "PL": ("dram", [DD, 128, 36], "int32"),
+    "XS": ("dram", [N * 128, QUART], "bfloat16"), "XL": ("dram", [N, 128, QUART], "bfloat16"),
+    "YL": ("dram", [R, 128, PIECE], "bfloat16"),
+    "LS": sb(DD * 36, "int32"), "LAi": sb(LC, "int32"), "LBi": sb(LC, "int32"),
+    "LA": sb(LC, "uint16"), "LB": sb(LC, "uint16"), "Zi": sb(LC, "int32"), "Li": sb(4, "int32"),
+    "ZB": sb(LC + 16, "bfloat16"),
+    "XA": sb(Z, "bfloat16"), "XB": sb(Z, "bfloat16"),
+    "GA": sb(Z, "bfloat16"), "GB": sb(Z, "bfloat16"), "QW": sb(Z, "float32"),
+    "PQ": sb(QUART, "float32"), "X": sb(QUART, "float32"), "RD": sb(QUART, "bfloat16"),
+    "IW": sb(2368, "bfloat16"), "W0": sb(Z, "bfloat16"), "ZW": sb(Z, "bfloat16"),
+    "KV": sb(QUART, "bfloat16"), "VAL": sb(QUART, "bfloat16"),
+    "Wa": sb(Z + 16, "bfloat16"), "Wb": sb(Z + 16, "bfloat16"), "W6": sb(Z + 16, "bfloat16"),
+    "G": sb(HALF, "bfloat16"), "TT": sb(Z, "bfloat16"), "G7": sb(QUART, "bfloat16"), "OUT": sb(HALF, "bfloat16"),
+    "L0": sb(72, "uint16"), "L1": sb(72, "uint16"), "LI": sb(36, "uint16"), "L7": sb(36, "uint16"),
+    "Lf0": sb(72, "float32"), "Lf1": sb(72, "float32"), "Lq": sb(72, "float32"),
+    "La": sb(48, "uint16"), "Lb": sb(48, "uint16"), "SEL": sb(8, "uint16"),
+    "ZL": sb(LC, "uint16"), "ZLf": sb(LC, "float32"), "KL": sb(36, "uint16"),
+    "pi0": sb(1, "int32"), "fi": sb(6, "int32"), "F": sb(6, "float32"), "Cc": sb(80, "float32"),
+    "C16": sb(LC, "float32"), "MT": sb(LC, "float32"), "INC": sb(40, "bfloat16"),
+    "Rx": sb(176, "bfloat16"), "TA": sb(128, "bfloat16"), "TB": sb(128, "bfloat16"), "TC": sb(128, "bfloat16"),
+    "TD": sb(128, "bfloat16"), "SU": sb(8, "bfloat16"),
+    "BP": sb(160, "bfloat16"), "BI": sb(160, "bfloat16"), "BR": sb(144, "bfloat16"), "BL": sb(176, "bfloat16"),
+    "ONES": sb(PIECE, "bfloat16"), "OFFM": sb(128, "bfloat16"),
+}
+for _m in ["M1", "MRB", "MA", "MB", "MRG", "NM", "RQ0", "RQ1", "RQ2", "RQ3", "PRE", "PREm", "PRE6",
+           "RP0", "RP1", "R60", "R61", "NEGI"]:
+    SCRATCH[_m] = sb(128, "bfloat16")
+for _m in ["EA", "EB"]:
+    SCRATCH[_m] = sb(176, "bfloat16")
+for _m in ["FA", "FB", "PK", "GP0", "GP1"]:
+    SCRATCH[_m] = sb(132, "bfloat16")
+for _b in range(8):
+    SCRATCH["b%d" % _b] = ("psum", [128, 512], "float32")
+
+NDMA = 40
+SEMAPHORES = (["sv", "ss", "sp", "sg", "sent", "hop"] + ["d%d" % i for i in range(NDMA)]
+              + ["al%d" % i for i in range(DD)] + ["ax%d" % i for i in range(N)] + ["ay%d" % i for i in range(R)])
+
+CALLS = [[(1, "self", 0), (2, "far", 0), (4, "far", 1)], [(3, "self", 0), (6, "far", 2), (7, "near", 0)], [(5, "self", 0)]]
+ARRIVAL = [1, 3, 5, 2, 4, 7, 6]
+
+
+def bits(engs):
+    m = 0
+    for e in engs:
+        m |= 1 << e
+    return m
+
+
+def send_steps(T, topo, q):
+    core = T.cores[q]
+    side = {"far": [c for c in topo.cores_of(core) if topo.die(c) != topo.die(core)],
+            "near": [c for c in topo.cores_of(core) if topo.die(c) == topo.die(core) and c != core]}
+    out = []
+    for call in CALLS:
+        used = []
+        for k, how, i in call:
+            if how == "self":
+                used += topo.engines(core, T.cores[(q + k) % N])
+        handed = [c for c in call if c[1] != "self"]
+        st = []
+        for k, how, i in call:
+            d = (q + k) % N
+            if how == "self":
+                st.append((d, T.cores[d], topo.engines(core, T.cores[d])))
+            else:
+                c = side[how][i]
+                free = [e for e in topo.engines(core, c) if e not in used]
+                n = len(free) // len(handed)
+                a = handed.index((k, how, i))
+                st.append((d, c, free[a * n:a * n + n]))
+        out.append(st)
+    return out
+
+
+def rank_program(g, core, T, topo):
+    q = T.rank_of(core)
+    if q is None:
+        for s in range(N):
+            for st in send_steps(T, topo, s):
+                for d, c, engs in st:
+                    if c == core:
+                        dst = T.cores[d]
+                        rid, pid = topo.addr(dst, core)
+                        g.wait_ge(T.sem.hop, len(engs))
+                        g.remote_dma(T.XL[s], T.XL[0], T.sem["ax%d" % s], T.sem.sent, pid, rid, topo.mask(core, dst))
+                        g.wait_ge(T.sem.sent, len(topo.engines(core, dst)))
+        return
+    z, h = q // R, q % R
+    ops = []
+
+    def add(queue, fn, r=(), w=(), kind="c", sem=None, n=0):
+        ops.append({"q": queue, "fn": fn, "r": list(r), "w": list(w), "kind": kind, "sem": sem, "n": n})
+
+    ndma = [0]
+
+    def dma(out, in_, r, w, queue="sync"):
+        eng = g.sync if queue == "sync" else g.scalar
+        add(queue, lambda: eng.dma_start(out, in_), r, w, "d", "d%d" % ndma[0], 16)
+        ndma[0] += 1
+
+    def landed(sem, n, key):
+        add(None, None, (), [key], "x", sem, n)
+
+    V = g.vector
+
+    def ts(out, in0, s1, s2, o0, o1, r, w):
+        if o1 is None:
+            add("v", lambda: V.tensor_scalar(out, in0, s1, None, o0), r, w)
+        else:
+            add("v", lambda: V.tensor_scalar(out, in0, s1, s2, o0, o1), r, w)
+
+    def tt(out, in0, in1, o, r, w):
+        add("v", lambda: V.tensor_tensor(out, in0, in1, o), r, w)
+
+    def cp(out, in_, r, w):
+        add("v", lambda: V.tensor_copy(out, in_), r, w)
+
+    def ms(ap, c, w):
+        add("v", lambda: V.memset(ap, c), (), w)
+
+    def act(out, in_, r, w, **kw):
+        add("s", lambda: g.scalar.activation(out, in_, Act.Identity, **kw), r, w)
+
+    def mm(out, lhsT, rhs, start, stop, r, bank):
+        add("p", lambda: g.tensor.matmul(out, lhsT, rhs, start, stop), r, [bank])
+
+    def iota(out, pattern, base, cm, w, small=True):
+        if small:
+            add("g", lambda: g.iota(out, pattern, base, cm, allow_small_or_imprecise_dtypes=True), (), w)
+        else:
+            add("g", lambda: g.iota(out, pattern, base, cm), (), w)
+
+    sent = [0]
+
+    def remote(transfers, r):
+        tr = []
+        for src, dst, c, engs, sem in transfers:
+            rid, pid = topo.addr(c, core)
+            tr.append(RemoteDMATransfer(dst_ids=[DstId(rid=rid, pnc=pid)], dma_engine_mask=bits(engs),
+                                        remote_sem=T.sem[sem], src=src, dst=dst))
+            sent[0] += len(engs)
+        add("g", lambda: g.remote_dma_fused(tr, local_sem=T.sem.sent), r, (), "r")
+
+    B = [T["b%d" % i] for i in range(8)]
+    bk = ["b%d" % i for i in range(8)]
+    rows = slice(32 * h, 32 * h + 32)
+    off_engs = topo.engines(core, T.cores[(q + 1) % N])
+    noff = len(off_engs)
+    order = [q] + [(q - k) % N for k in ARRIVAL]
+    data = [s for s in order if s < DD]
+    tiles = {"A": order[:4], "B": order[4:]}
+    chunk = lambda c: slice(CH * c, CH * c + CH)
+    piece = lambda c: slice(PIECE * c, PIECE * c + PIECE)
+    j0 = lambda s4: HALF * (s4 % 2) + QUART * (s4 // 2)
+
+    if q < DD:
+        dma(T.PS[0:512, :], T.pi[:, 0:LC], (), ["PS0"], "sync")
+        dma(T.PS[512:1024, :], T.pi[:, LC:2 * LC], (), ["PS1"], "scalar")
+    dma(T.Zi[0:32, :], T.zero[rows, :], (), ["Zi"], "scalar")
+    dma(T.Li[0:32, 0:2], T.lost[rows, :], (), ["Li"], "scalar")
+    steps = send_steps(T, topo, q)
+    for st in steps:
+        for d, c, engs in st:
+            dma(T.XS[128 * d:128 * d + 128, :], T.x[32 * (d % R):32 * (d % R) + 32, Z * (d // R):Z * (d // R) + Z], (), ["XS%d" % d])
+    iota(T.pi0[:], [[0, 1]], 0, 1, ["pi0"], False)
+    iota(T.TA[:], [[16, 2], [0, 4], [1, 16]], 0, 0, ["TA"])
+    iota(T.Rx[:], [[1, 176]], -48, 0, ["Rx"])
+    iota(T.C16[:], [[16, LC]], 0, 0, ["C16"])
+    iota(T.TB[:], [[0, 4], [1, 32]], 0, 0, ["TB"])
+    iota(T.TD[:], [[64, 2], [0, 4], [1, 16]], 0, 0, ["TD"])
+    if q < DD:
+        remote([(T.PS[128 * d:128 * d + 128, :], T.PL[q], T.cores[d], [off_engs[i]], "al%d" % q)
+                for i, d in enumerate([(q + k) % N for k in range(1, N)])], ["PS0", "PS1"])
+    for st in steps:
+        remote([(T.XS[128 * d:128 * d + 128, :], T.XL[q if c == T.cores[d] else 0], c, engs,
+                 "ax%d" % q if c == T.cores[d] else "hop") for d, c, engs in st], ["XS%d" % d for d, c, engs in st])
+    iota(T.TC[:], [[32, 4], [0, 2], [1, 16]], 0, 0, ["TC"])
+    iota(T.SU[:], [[64, 2], [0, 2], [16, 2]], 0, 0, ["SU"])
+    for s in range(N):
+        if s != q:
+            landed("ax%d" % s, noff, "XL%d" % s)
+            if s < DD:
+                landed("al%d" % s, 1, "PL%d" % s)
+    for s in range(R):
+        if s != h:
+            landed("ay%d" % s, noff, "YL%d" % s)
+
+    def lists_of(s):
+        return (T.pi[rows, LC * z:LC * z + LC], []) if s == q else (T.PL[s], ["PL%d" % s])
+
+    def place(s):
+        src, r = (T.x[rows, Z * z:Z * z + Z], []) if s == q else (T.XL[s], ["XL%d" % s])
+        t, i = "AB"[order.index(s) // 4], order.index(s) % 4
+        dma(T["X" + t][32 * i:32 * i + 32, :], src, r, ["X%s%d" % (t, i)])
+
+    place(q)
+    for s in data:
+        src, r = lists_of(s)
+        dma(T.LS[:, 36 * s:36 * s + 36], src, r, ["LS%d" % s])
+    for s in data:
+        src, r = lists_of(s)
+        t, i = "AB"[order.index(s) // 4], order.index(s) % 4
+        dma(T["L%si" % t][32 * i:32 * i + 32, :], src, r, ["L%si%d" % (t, i)])
+    for s in order[1:]:
+        place(s)
+    kLS = ["LS%d" % s for s in range(DD)]
+    kX = {t: ["X%s%d" % (t, i) for i in range(4)] for t in "AB"}
+
+    ms(T.ZW[:], 0.0, ["ZW"])
+    fields = {"p": 127, "p32": 31, "r": 15, "u64": 64, "p3": 3, "e16": 16}
+    F = {}
+    for i, name in enumerate(fields):
+        ts(T.fi[:, i:i + 1], T.pi0[:], fields[name], None, Op.bitwise_and, None, ["pi0"], ["fi%d" % i])
+        F[name] = T.F[:, i:i + 1]
+    cp(T.F[:], T.fi[:], ["fi%d" % i for i in range(6)], ["F"])
+    for nm in ["BP", "BI", "BR", "BL"]:
+        ms(T[nm][:], 0.0, [nm])
+    ncol = [0]
+    C = {}
+    at = {}
+
+    def slot(name, n=1):
+        at[name] = ncol[0]
+        C[name] = T.Cc[:, ncol[0]:ncol[0] + n]
+        ncol[0] += n
+
+    def col(name, in0, s1, s2, o0, o1, r, n=1):
+        slot(name, n)
+        ts(C[name], in0, s1, s2, o0, o1, ["F"] + r, [name])
+
+    def lin(name, in0, scale, bias, r, n=1):
+        slot(name, n)
+        act(C[name], in0, ["F"] + r, [name], scale=scale, bias=bias)
+
+    def e(name, i):
+        return T.Cc[:, at[name] + i:at[name] + i + 1]
+
+    def mat(name, table, tkey, code, wgt, r, o1=Op.mult, out=None):
+        ts(T[name][:] if out is None else out, table, code, wgt, Op.is_equal, o1 if wgt is not None else None,
+           ["F", tkey] + r, [name])
+
+    lin("p63", F["u64"], -1.0, F["p"], [])
+    lin("cE", F["e16"], 4.0, F["r"], [])
+    lin("p60", F["p3"], -1.0, C["p63"], ["p63"])
+    lin("p48", F["r"], -1.0, C["p63"], ["p63"])
+    lin("kc0", C["p60"], 0.25, 0.0, ["p60"])
+    lin("k32", F["p32"], -1.0, C["p63"], ["p63"])
+    lin("kc", F["p3"], float(QUART), C["kc0"], ["kc0"])
+    lin("cTC", F["e16"], -1.0, F["p"], [])
+    lin("cTD", F["u64"], 1.0, F["r"], [])
+    lin("p80", F["u64"], 1.0, F["e16"], [])
+    lin("cF", F["p32"], 4.0, 0.0, [])
+    lin("cK", F["r"], 4.0, F["u64"], [])
+    lin("we1", F["e16"], 1.0 / 16.0, 0.0, [])
+    lin("we0", F["e16"], -1.0 / 16.0, 1.0, [])
+    lin("c32", C["cTD"], 1.0, 32.0, ["cTD"])
+    lin("c80", C["p80"], 1.0, 32.0, ["p80"])
+    lin("ck", C["k32"], 1.0 / 32.0, 0.0, ["k32"])
+    lin("cd", C["k32"], -1.0 / 32.0, 1.0, ["k32"])
+    lin("cb", C["k32"], OFFSET / 32.0, 0.0, ["k32"])
+    lin("cG", C["k32"], 1.0 / 16.0, C["cK"], ["k32", "cK"])
+    slot("disk", 2)
+    kD = []
+    for n, t in enumerate("AB"):
+        for i in range(4):
+            ms(T.Cc[32 * i:32 * i + 32, at["disk"] + n:at["disk"] + n + 1], float(tiles[t][i]), ["disk%d" % (4 * n + i)])
+            kD.append("disk%d" % (4 * n + i))
+    col("e5", T.Rx[:, 48:53], F["r"], None, Op.is_equal, None, ["Rx"], 5)
+    mat("M1", T.TA[:], "TA", F["p32"], None, [])
+    col("m01", F["r"], 2.0, None, Op.is_lt, None, [])
+    col("hi", e("e5", 0), e("e5", 3), 4.0, Op.add, Op.mult, ["e5"])
+    col("lo", e("e5", 1), e("e5", 4), None, Op.add, None, ["e5"])
+    col("c256", e("e5", 2), 256.0, None, Op.mult, None, ["e5"])
+    ts(T.MT[:], T.C16[:], F["r"], None, Op.add, None, ["C16", "F"], ["MT"])
+    ts(T.INC[:], T.C16[:, 0:40], C["hi"], None, Op.mult, None, ["C16", "hi"], ["INC"])
+    ts(T.IW[:, 0:64], T.Rx[:, 48:112], C["lo"], C["c256"], Op.mult, Op.add, ["Rx", "lo", "c256"], ["IW"])
+    ts(T.ZB[0:32, 0:LC], T.Zi[0:32, :], float(Z), None, Op.mult, None, ["Zi"], ["ZB0"])
+    cp(T.ZB[0:32, LC:LC + 2], T.Li[0:32, 0:2], ["Li"], ["ZB1"])
+    mm(B[6][:, 0:LC + 2], T.M1[0:32, :], T.ZB[0:32, 0:LC + 2], True, True, ["M1", "ZB0", "ZB1"], bk[6])
+
+    def grow(s):
+        n = 64 << s
+        m = min(n, 2368 - n)
+        ts(T.IW[:, n:n + m], T.IW[:, 0:m], T.INC[:, 1 << s:(1 << s) + 1], None, Op.add, None, ["IW", "INC"], ["IW"])
+
+    grow(0)
+    col("m234", e("e5", 2), e("e5", 3), e("e5", 4), Op.add, Op.add, ["e5"])
+    grow(1)
+    col("wq", T.C16[:, 0:4], C["p48"], None, Op.is_equal, None, ["C16", "p48"], 4)
+    grow(2)
+    tt(T.ZLf[:], T.MT[:], B[6][:, 0:LC], Op.max, ["MT", bk[6]], ["ZLf"])
+    grow(3)
+    ts(T.KL[:], T.C16[:, 0:36], C["kc"], None, Op.add, None, ["C16", "kc"], ["KL"])
+    grow(4)
+    cp(T.ZL[:], T.ZLf[:], ["ZLf"], ["ZL"])
+    grow(5)
+    lin("m34", e("e5", 3), 1.0, e("e5", 4), ["e5"])
+    lin("mptr", C["ck"], C["m01"], 0.0, ["m01", "ck"])
+    lin("nq", C["wq"], -1.0, 0.0, ["wq"], 4)
+    lin("wp0", e("wq", 2), C["m01"], e("wq", 0), ["wq", "m01"])
+    lin("wp1", e("wq", 3), C["m01"], e("wq", 1), ["wq", "m01"])
+    lin("nptr", C["mptr"], -1.0, 0.0, ["mptr"])
+    iw = T.IW[:, 0:2368]
+    act(T.W0[:, HALF:Z], iw.indirect(T.ZL[:, 72:144]), ["IW", "ZL", "m01"], ["W0b"], scale=C["m01"])
+    act(T.KV[:], iw.indirect(T.KL[:]), ["IW", "KL", "m234"], ["KV"], scale=C["m234"])
+    col("ab36", B[6][:, LC:LC + 2], 36.0, None, Op.mult, None, [bk[6]], 2)
+    mat("MRB", T.TB[:], "TB", F["p"], None, [])
+    mm(B[7][:, 0:2], T.MRB[0:32, :], T.ZB[0:32, LC:LC + 2], True, True, ["MRB", "ZB1"], bk[7])
+    ts(T.W0[:, 0:HALF], iw.indirect(T.ZL[:, 0:72]), C["m01"], None, Op.mult, None, ["IW", "ZL", "m01"], ["W0a"])
+    ts(T.SEL[:, 0:3], T.MT[:, 0:3], 35.0, e("ab36", 0), Op.min, Op.add, ["MT", "ab36"], ["SELa"])
+    ts(T.SEL[:, 4:7], T.MT[:, 0:3], 35.0, e("ab36", 1), Op.min, Op.add, ["MT", "ab36"], ["SELb"])
+    col("baseQ", C["disk"], float(DD - 1), float(DD), Op.max, Op.subtract, kD, 2)
+    col("isP", C["disk"], float(DD), 2.0, Op.is_equal, Op.mult, kD, 2)
+    col("isQ", C["disk"], float(DD + 1), 1.0, Op.is_equal, Op.subtract, kD, 2)
+    col("qA", B[7][:, 0:2], e("disk", 0), None, Op.is_equal, None, [bk[7]] + kD, 2)
+    col("qB", B[7][:, 0:2], e("disk", 1), None, Op.is_equal, None, [bk[7]] + kD, 2)
+    slot("baseP", 2)
+    tt(C["baseP"], C["isP"], C["isQ"], Op.add, ["isP", "isQ"], ["baseP"])
+    mat("BP", T.TD[:, 0:128:32], "TD", F["u64"], C["m01"], ["m01", "BP"], out=T.BP[:, 31:128:32])
+    mat("BI", T.TD[:, 0:128:32], "TD", F["u64"], C["m34"], ["m34", "BI"], out=T.BI[:, 31:128:32])
+    for n, t in enumerate("AB"):
+        col("wQ" + t, e("q" + t, 0), e("q" + t, 1), e("baseQ", n), Op.add, Op.add, ["q" + t, "baseQ"])
+        col("wP" + t, e("q" + t, 0), e("q" + t, 1), e("baseP", n), Op.add, Op.add, ["q" + t, "baseP"])
+        for i, s in enumerate(tiles[t]):
+            if s >= DD:
+                cp(T["L%si" % t][32 * i:32 * i + 32, :], T.MT[32 * i:32 * i + 32, :], ["MT"], ["L%si%d" % (t, i)])
+    f131 = T.Rx[:, 45:176]
+    diag = T.Rx[:, 48:176]
+    for t in "AB":
+        mat("E" + t, T.Rx[:], "Rx", C["cE"], C["wP" + t], ["wP" + t, "cE"])
+        mat("M" + t, T.TA[:], "TA", F["p32"], C["wQ" + t], ["wQ" + t])
+
+    cp(T.La[:], T.LS[:].indirect(T.SEL[:, 0:3]), kLS + ["SELa"], ["La"])
+    cp(T.Lb[:], T.LS[:].indirect(T.SEL[:, 4:7]), kLS + ["SELb"], ["Lb"])
+    act(T.VAL[:, piece(1)], T.W0[:].indirect(T.La[:, 18:36]), ["W0a", "W0b", "La"], ["VAL1"])
+    cp(T.VAL[:, piece(0)], T.W0[:].indirect(T.La[:, 0:18]), ["W0a", "W0b", "La"], ["VAL0"])
+    cp(T.LA[:], T.LAi[:], ["LAi%d" % i for i in range(4)], ["LA"])
+    cp(T.LB[:], T.LBi[:], ["LBi%d" % i for i in range(4)], ["LB"])
+    tt(T.ZW[:].indirect(T.Lb[:, 0:36]), T.VAL[:], T.KV[:], Op.add, ["VAL0", "VAL1", "KV", "Lb", "ZW"], ["ZW"])
+
+    def half_lists(nm, b):
+        for eta in range(2):
+            for rho in range(16):
+                x0 = 15 - rho + 16 - 16 * eta
+                mm(B[b][:, CH:CH + 72], T[nm][:, x0:x0 + 128], T.ZW[:, HALF * eta + rho:HALF * eta + HALF:16],
+                   eta == 0 and rho == 0, eta == 1 and rho == 15, [nm, "ZW"], bk[b])
+
+    def p_quarter(t):
+        for c in range(2):
+            for s4 in range(4):
+                a = j0(s4) + PIECE * c
+                mm(B[6 + c][:, 0:PIECE], T["E" + t][:, 48 - 16 * s4:176 - 16 * s4], T["X" + t][:, a:a + PIECE],
+                   t == "A" and s4 == 0, t == "B" and s4 == 3, kX[t] + ["E" + t], bk[6 + c])
+
+    def p_final(t):
+        for eta in range(2):
+            for t4 in range(4):
+                a = HALF * eta + PIECE * t4
+                mm(B[6 + eta][:, 0:PIECE], T["F" + t][:, 3 - t4:131 - t4], T["X" + t][:, a:a + PIECE], False, False,
+                   kX[t] + ["F" + t], bk[6 + eta])
+
+    half_lists("BI", 5)
+    p_quarter("A")
+    cut = 960
+    act(T.GA[:, cut:Z], T.XA[:].indirect(T.LA[:, cut // 16:LC]), kX["A"] + ["LA"], ["GA1"])
+    cp(T.GA[:, 0:cut], T.XA[:].indirect(T.LA[:, 0:cut // 16]), kX["A"] + ["LA"], ["GA0"])
+    ts(T.Lq[:, 0:36], B[5][:, CH:CH + 36], C["cd"], None, Op.mult, None, [bk[5], "cd"], ["Lq0"])
+    ts(T.Lq[:, 36:72], B[5][:, CH + 36:CH + 72], C["ck"], None, Op.mult, None, [bk[5], "ck"], ["Lq1"])
+    col("m012", F["r"], 3.0, None, Op.is_lt, None, [])
+    tt(T.Lf1[:, 0:36], T.Lq[:, 0:36], T.Lq[:, 36:72], Op.add, ["Lq0", "Lq1"], ["Lf1"])
+    col("c34", F["p"], 34.0, OFFSET / 256.0, Op.is_equal, Op.mult, [])
+    mat("NM", diag, "Rx", F["p"], C["nptr"], ["nptr"])
+    cp(T.LI[:], T.Lf1[:, 0:36], ["Lf1"], ["LI"])
+    mat("MRG", T.TC[:], "TC", C["c32"], C["m012"], ["c32", "m012"])
+    for s4 in range(4):
+        mat("RQ%d" % s4, T.TC[:], "TC", C["cTD"], e("nq", s4), ["nq", "cTD"])
+    for c in range(6):
+        mm(B[c][:, 0:CH], T.MA[:], T.GA[:, chunk(c)], True, False,
+           ["MA"] + [["GA0"], ["GA0"], ["GA0", "GA1"], ["GA1"], ["GA1"], ["GA1"]][c], bk[c])
+    p_quarter("B")
+    for c in range(3):
+        act(T.GB[:, chunk(c + 3)], T.XB[:].indirect(T.LB[:, 24 * c + 72:24 * c + 96]), kX["B"] + ["LB"], ["GB%d" % (c + 3)])
+        cp(T.GB[:, chunk(c)], T.XB[:].indirect(T.LB[:, 24 * c:24 * c + 24]), kX["B"] + ["LB"], ["GB%d" % c])
+        for cc in [c, c + 3]:
+            mm(B[cc][:, 0:CH], T.MB[:], T.GB[:, chunk(cc)], False, True, ["MB", "GB%d" % cc], bk[cc])
+    for c in range(3):
+        cp(T.QW[:, chunk(c)], B[c][:, 0:CH], [bk[c]], ["QW%d" % c])
+        act(T.QW[:, chunk(c + 3)], B[c + 3][:, 0:CH], [bk[c + 3]], ["QW%d" % (c + 3)])
+    cp(T.PQ[:, piece(0)], B[6][:, 0:PIECE], [bk[6]], ["PQ0"])
+    act(T.PQ[:, piece(1)], B[7][:, 0:PIECE], [bk[7]], ["PQ1"])
+    kQW = ["QW%d" % c for c in range(6)]
+    for nm in ["Wa", "Wb", "W6"]:
+        act(T[nm][:, Z:Z + 16], T.TA[:, 0:16], ["TA"], [nm + "s"], scale=0.0)
+    act(T.ONES[0:32, :], T.IW[0:32, 0:PIECE], ["IW"], ["ONES"], scale=0.0, bias=1.0)
+    act(T.OFFM[0:32, :], T.TA[0:32, :], ["TA"], ["OFFM"], scale=0.0, bias=OFFSET / 32.0)
+
+    def parts(c):
+        a = CH * (c % 3)
+        return [(a, a + CH)] if c % 3 != 1 else [(a, QUART), (QUART, a + CH)]
+
+    def pointers(c, lo, hi):
+        a, j = CH * (c % 3), HALF * (c // 3)
+        mm(B[c][:, lo - a:hi - a], T.MRG[:], T.ZW[:, j + lo:j + hi], True, False, ["MRG", "ZW"], bk[c])
+        mm(B[c][:, lo - a:hi - a], T.NM[:], T.IW[:, j + lo:j + hi], False, False, ["NM", "IW"], bk[c])
+
+    half_lists("BP", 2)
+    for c in [0, 3, 2, 5, 1, 4]:
+        pointers(c, *parts(c)[0])
+    for c in range(2):
+        tt(T.X[:, piece(c)], T.QW[:].indirect(T.LI[:, 18 * c:18 * c + 18]), T.PQ[:, piece(c)], Op.subtract,
+           kQW + ["LI", "PQ%d" % c], ["X%d" % c])
+    for c in range(2):
+        ts(B[6 + c][:, 0:PIECE], T.X[:, piece(c)], MAGIC, MAGIC, Op.add, Op.subtract, ["X%d" % c], [bk[6 + c]])
+    for c in range(2):
+        tt(T.RD[:, piece(c)], T.X[:, piece(c)], B[6 + c][:, 0:PIECE], Op.subtract, ["X%d" % c, bk[6 + c]], ["RD%d" % c])
+    mat("PRE", diag, "Rx", F["p"], None, [])
+    mat("RP0", T.TC[:], "TC", C["cTC"], C["wp0"], ["wp0", "cTC"])
+    mat("RP1", T.TC[:], "TC", C["cTC"], C["wp1"], ["wp1", "cTC"])
+    for c in [0, 3, 2, 5, 1, 4]:
+        eta, a = c // 3, CH * (c % 3)
+        for i, (lo, hi) in enumerate(parts(c)):
+            kap = lo // QUART
+            if i:
+                pointers(c, lo, hi)
+            nm = "RQ%d" % (2 * kap + eta)
+            mm(B[c][:, lo - a:hi - a], T[nm][:], T.RD[:, lo - QUART * kap:hi - QUART * kap], False, True, [nm, "RD0", "RD1"], bk[c])
+    for eta in range(2):
+        mm(B[6 + eta][:, 0:PIECE], T.OFFM[0:32, :], T.ONES[0:32, :], True, False, ["OFFM", "ONES"], bk[6 + eta])
+    for c in [0, 2, 1]:
+        if c == 1:
+            cp(T.L0[:], B[2][:, CH:CH + 72], [bk[2]], ["L0"])
+            cp(T.Lf0[:], B[2][:, CH:CH + 72], [bk[2]], ["Lf0"])
+            mat("BR", T.SU[:], "SU", C["p80"], C["mptr"], ["mptr", "BR", "p80"], out=T.BR[:, 15:128:16])
+            act(T.PREm[:], T.PRE[:], ["PRE", "c34"], ["PREm"], bias=C["c34"])
+        cp(T.Wa[:, chunk(c)], B[c][:, 0:CH], [bk[c]], ["Wa%d" % c])
+        act(T.Wa[:, chunk(c + 3)], B[c + 3][:, 0:CH], [bk[c + 3]], ["Wa%d" % (c + 3)])
+
+    def spare(rd):
+        if rd == 1:
+            mat("FA", f131, "Rx", C["cF"], C["wPA"], ["cF", "wPA"], out=T.FA[:, 0:131])
+            mat("FB", f131, "Rx", C["cF"], C["wPB"], ["cF", "wPB"], out=T.FB[:, 0:131])
+            mat("GP0", T.Rx[:, 47:176], "Rx", C["cG"], C["we0"], ["cG", "we0"], out=T.GP0[:, 0:129])
+            act(T.NEGI[:], T.PRE[:], ["PRE"], ["NEGI"], scale=-1.0)
+        if rd == 3:
+            mat("PRE6", T.TD[:], "TD", F["p"], C["c34"], ["c34"], o1=Op.add)
+            mat("R60", T.TD[:], "TD", C["cTD"], e("wq", 0), ["wq", "cTD"])
+            mat("R61", T.TD[:], "TD", C["cTD"], e("wq", 1), ["wq", "cTD"])
+        if rd == 5:
+            mat("BL", T.C16[:, 0:11], "C16", C["c80"], C["mptr"], ["c80", "mptr", "BL"], out=T.BL[:, 15:176:16])
+            mat("PK", f131, "Rx", C["cK"], e("wq", 0), ["cK", "wq"], out=T.PK[:, 0:131])
+            mat("GP1", T.Rx[:, 47:176], "Rx", C["cG"], C["we1"], ["cG", "we1"], out=T.GP1[:, 0:129])
+
+    names = ["Wa", "Wb", "Wa", "Wb", "Wa", "Wb", "W6"]
+    for rd in range(1, 7):
+        wn, nn = names[rd - 1], names[rd]
+        W, Wn = T[wn], T[nn]
+        ln, lnn = "L%d" % ((rd - 1) % 2), "L%d" % (rd % 2)
+        lf, lfn = "Lf%d" % ((rd - 1) % 2), "Lf%d" % (rd % 2)
+        kW = [wn + str(c) for c in range(6)] + [wn + "s", ln]
+        for c in range(3):
+            a = CH * c
+            if c < 2 or rd % 2:
+                act(T.G[:, a + CH // 2:a + CH], W[:].indirect(T[ln][:, 24 * c + 12:24 * c + 24]), kW, ["G%db" % c])
+                cp(T.G[:, a:a + CH // 2], W[:].indirect(T[ln][:, 24 * c:24 * c + 12]), kW, ["G%da" % c])
+            else:
+                cp(T.G[:, a:a + CH], W[:].indirect(T[ln][:, 24 * c:24 * c + 24]), kW, ["G2a", "G2b"])
+        kG = [["G%da" % c, "G%db" % c] for c in range(3)]
+        allG = kG[0] + kG[1] + kG[2]
+        pre = "PRE6" if rd == 6 else "PREm" if rd % 2 == 0 else "PRE"
+        rep = "R6" if rd == 6 else "RP"
+        own = lambda c: rd % 2 == 0 or c >= 3
+
+        def old(c):
+            if own(c):
+                mm(B[c][:, 0:CH], T[pre][:], W[:, chunk(c)], True, False, [pre, wn + str(c)], bk[c])
+
+        def new(c):
+            nm = rep + str(c // 3)
+            mm(B[c][:, 0:CH], T[nm][:], T.G[:, chunk(c % 3)], not own(c), True, [nm] + kG[c % 3], bk[c])
+
+        lb = 2 * (rd % 2)
+
+        def convert():
+            if rd < 6:
+                for rho in range(16):
+                    mm(B[lb][:, CH:CH + 72], T.BR[:, 15 - rho:143 - rho], T.G[:, rho:HALF:16], rho == 0, rho == 15,
+                       ["BR"] + allG, bk[lb])
+            else:
+                for kap in range(2):
+                    for rho in range(16):
+                        x0 = 15 - rho + 32 - 32 * kap
+                        mm(B[0][:, CH:CH + 36], T.BL[:, x0:x0 + 128], T.G[:, QUART * kap + rho:QUART * kap + QUART:16],
+                           kap == 0 and rho == 0, kap == 1 and rho == 15, ["BL"] + allG, bk[0])
+
+        def take_list():
+            if rd < 6:
+                tt(T[lfn][:], B[lb][:, CH:CH + 72], T[lf][:], Op.add, [bk[lb], lf], [lfn])
+            else:
+                tt(T.Lf0[:, 0:36], B[0][:, CH:CH + 36], T.Lf0[:, 36:72], Op.add, [bk[0], "Lf0"], ["Lf7"])
+
+        def narrow_list():
+            if rd < 6:
+                cp(T[lnn][:], T[lfn][:], [lfn], [lnn])
+            else:
+                cp(T.L7[:], T.Lf0[:, 0:36], ["Lf7"], ["L7"])
+
+        if rd % 2:
+            for c in [3, 4, 5]:
+                old(c)
+            for c in [0, 3, 1, 4]:
+                new(c)
+            convert()
+            new(2)
+            new(5)
+            for c in range(3):
+                if c == 2:
+                    spare(rd)
+                    take_list()
+                tt(Wn[:, chunk(c)], B[c][:, 0:CH], W[:, chunk(c)], Op.add, [bk[c], wn + str(c)], [nn + str(c)])
+                act(Wn[:, chunk(c + 3)], B[c + 3][:, 0:CH], [bk[c + 3]], [nn + str(c + 3)])
+            narrow_list()
+        else:
+            for c in range(3):
+                old(c)
+                old(c + 3)
+                new(c)
+                new(c + 3)
+            for i, c in enumerate([0, 3, 1, 4, 2, 5]):
+                if rd < 6:
+                    act(T.TT[:, chunk(c)], B[c][:, 0:CH], [bk[c], "cd", "cb"], ["TT%d" % c], scale=C["cd"], bias=C["cb"])
+                else:
+                    act(T.TT[:, chunk(c)], B[c][:, 0:CH], [bk[c]], ["TT%d" % c])
+                tt(Wn[:, chunk(c)], B[c][:, 0:CH], T.TT[:, chunk(c)], Op.subtract, [bk[c], "TT%d" % c], [nn + str(c)])
+                if i == 0:
+                    convert()
+                    if rd < 6:
+                        p_final("AB"[rd // 2 - 1])
+                if i == 1 and rd == 6:
+                    act(T.Lq[:, 0:36], T.Lf1[:, 0:36], ["Lf1", "cd"], ["Lq0"], scale=C["cd"])
+                    act(T.Lq[:, 36:72], T.Lf1[:, 36:72], ["Lf1", "ck"], ["Lq1"], scale=C["ck"])
+                if i == 2 and rd == 6:
+                    tt(T.Lf0[:, 36:72], T.Lq[:, 0:36], T.Lq[:, 36:72], Op.add, ["Lq0", "Lq1"], ["Lf0"])
+                if i == 3:
+                    take_list()
+                if i == 4:
+                    narrow_list()
+
+    kW = ["W6%d" % c for c in range(6)]
+    bank = [3, 1, 6, 7]
+    for eta in range(2):
+        mm(B[bank[eta]][:, 0:PIECE], T.OFFM[0:32, :], T.ONES[0:32, :], True, False, ["OFFM", "ONES"], bk[bank[eta]])
+    act(T.G7[:, piece(1)], T.W6[:].indirect(T.L7[:, 18:36]), kW + ["W6s", "L7"], ["G71"])
+    cp(T.G7[:, piece(0)], T.W6[:].indirect(T.L7[:, 0:18]), kW + ["W6s", "L7"], ["G70"])
+    for t4 in range(4):
+        for eta in range(2):
+            a = HALF * eta + PIECE * t4
+            mm(B[bank[eta]][:, 0:PIECE], T.PK[:, 3 - t4:131 - t4], T.W6[:, a:a + PIECE], False, False,
+               kW[a // CH:(a + PIECE - 1) // CH + 1] + ["PK"], bk[bank[eta]])
+    for eta in range(2):
+        for eps in range(2):
+            mm(B[bank[eta]][:, 0:PIECE], T["GP%d" % eta][:, 1 - eps:129 - eps], T.G7[:, piece(eps)],
+               False, eps == 1, ["GP%d" % eta, "G7%d" % eps], bk[bank[eta]])
+    for s in range(R):
+        b = bank[s]
+        act(T.TT[:, piece(s)], B[b][:, 0:PIECE], [bk[b]], ["TT0", "TT1", "TT2", "TF%d" % s], bias=-127.5)
+        tt(T.OUT[:, piece(s)], B[b][:, 0:PIECE], T.TT[:, piece(s)], Op.subtract, [bk[b], "TF%d" % s], ["OUT%d" % s])
+        if s < 2:
+            mm(B[6 + s][:, 0:PIECE], T.NEGI[:], T.OUT[:, piece(s)], False, True, ["NEGI", "OUT%d" % s], bk[6 + s])
+        if s == h:
+            dma(T.y[rows, :], T.OUT[:, piece(s)], ["OUT%d" % s], ["y%d" % s])
+        else:
+            remote([(T.OUT[:, piece(s)], T.YL[h], T.cores[R * z + s], off_engs, "ay%d" % h)], ["OUT%d" % s])
+    for s in range(R):
+        if s != h:
+            dma(T.y[32 * s:32 * s + 32, :], T.YL[s], ["YL%d" % s], ["y%d" % s], "scalar" if (s - h) % R == 2 else "sync")
+
+    emit(g, T, ops, sent[0])
+
+
+def emit(g, T, ops, sent):
+    queues = {"v": g.vector, "s": g.scalar, "scalar": g.scalar, "p": g.tensor, "g": g, "sync": g.sync}
+    same = {"scalar": "s"}
+    csem = {"v": "sv", "s": "ss", "p": "sp", "g": "sg"}
+    writer, readers = {}, {}
+    for i, o in enumerate(ops):
+        deps = set()
+        me = same.get(o["q"], o["q"])
+        far = lambda j: ops[j]["kind"] != "c" or o["kind"] != "c" or same.get(ops[j]["q"], ops[j]["q"]) != me
+        for k in o["r"]:
+            if k in writer:
+                deps.add(writer[k])
+            if k[0] == "b" and k[1:].isdigit():
+                deps.update(j for j in readers.get(k, []) if far(j))
+        for k in o["w"]:
+            if k in writer and far(writer[k]):
+                deps.add(writer[k])
+            deps.update(j for j in readers.get(k, []) if far(j))
+        for k in o["r"]:
+            readers.setdefault(k, []).append(i)
+        for k in o["w"]:
+            writer[k] = i
+            readers[k] = []
+        o["deps"] = deps
+    seen = {}
+    for o in ops:
+        me = same.get(o["q"], o["q"])
+        best = {}
+        for j in o["deps"]:
+            d = ops[j]
+            s = csem[d["q"]] if d["kind"] == "c" else d["sem"]
+            best[s] = max(best.get(s, -1), j)
+        o["waits"] = []
+        for s in sorted(best):
+            if seen.get((me, s), -1) < best[s]:
+                seen[(me, s)] = best[s]
+                o["waits"].append((s, best[s]))
+                ops[best[s]]["flag"] = True
+    count = {}
+    waited = set()
+    for o in ops:
+        if o["kind"] == "x":
+            o["val"] = o["n"]
+            continue
+        eng = queues[o["q"]]
+        for s, j in o["waits"]:
+            eng.wait_ge(T.sem[s], ops[j]["val"])
+            waited.add(s)
+        ins = o["fn"]()
+        if o["kind"] == "d":
+            ins.then_inc(T.sem[o["sem"]], 16)
+            o["val"] = 16
+        elif o["kind"] == "c" and o.get("flag"):
+            s = csem[o["q"]]
+            count[s] = count.get(s, 0) + 1
+            ins.then_inc(T.sem[s], 1)
+            o["val"] = count[s]
+    g.wait_ge(T.sem.sent, sent)
+    for o in ops:
+        if o["kind"] in "dx" and o["sem"] not in waited:
+            g.sync.wait_ge(T.sem[o["sem"]], o["n"])

@@ -2,10 +2,17 @@ from concourse.bass import DstId, RemoteDMATransfer
 from concourse.mybir import AluOpType as Op, ActivationFunctionType as Act
 
 N, R, Z, DD = 8, 4, 2304, 6
-HALF, QUART, PIECE, CH = Z // 2, Z // 4, Z // 8, Z // 6
+HALF, QUART, PIECE = Z // 2, Z // 4, Z // 8
 LC = Z // 16
+HALO = 128
 OFFSET = 49152.0
 MAGIC = 3221225472.0
+FLOOR = 33024
+U = 296
+K2 = 11 * U // 2 + 144
+DUMP = 12 * U
+ROUNDS = 7
+FIRST = 256
 
 
 def sb(cols, dtype):
@@ -16,43 +23,45 @@ SCRATCH = {
     "PS": ("dram", [N * 128, 36], "int32"), "PL": ("dram", [DD, 128, 36], "int32"),
     "XS": ("dram", [N * 128, QUART], "bfloat16"), "XL": ("dram", [N, 128, QUART], "bfloat16"),
     "YL": ("dram", [R, 128, PIECE], "bfloat16"),
-    "LS": sb(DD * 36, "int32"), "LAi": sb(LC, "int32"), "LBi": sb(LC, "int32"),
+    "LAi": sb(LC, "int32"), "LBi": sb(LC, "int32"), "LAh": sb(LC, "float16"), "LBh": sb(LC, "float16"),
+    "SaA": sb(228, "float16"), "SaB": sb(228, "float16"), "SbA": sb(228, "float16"), "SbB": sb(228, "float16"),
     "LA": sb(LC, "uint16"), "LB": sb(LC, "uint16"), "Zi": sb(LC, "int32"), "Li": sb(4, "int32"),
-    "ZB": sb(LC + 16, "bfloat16"),
-    "XA": sb(Z, "bfloat16"), "XB": sb(Z, "bfloat16"),
+    "ZB": sb(LC + 16, "bfloat16"), "XA": sb(Z, "bfloat16"), "XB": sb(Z, "bfloat16"),
     "GA": sb(Z, "bfloat16"), "GB": sb(Z, "bfloat16"), "QW": sb(Z, "float32"),
-    "PQ": sb(QUART, "float32"), "X": sb(QUART, "float32"), "RD": sb(QUART, "bfloat16"),
-    "IW": sb(2368, "bfloat16"), "W0": sb(Z, "bfloat16"), "ZW": sb(Z, "bfloat16"),
-    "KV": sb(QUART, "bfloat16"), "VAL": sb(QUART, "bfloat16"),
-    "Wa": sb(Z + 16, "bfloat16"), "Wb": sb(Z + 16, "bfloat16"), "W6": sb(Z + 16, "bfloat16"),
-    "G": sb(HALF, "bfloat16"), "TT": sb(Z, "bfloat16"), "G7": sb(QUART, "bfloat16"), "OUT": sb(HALF, "bfloat16"),
-    "L0": sb(72, "uint16"), "L1": sb(72, "uint16"), "LI": sb(36, "uint16"), "L7": sb(36, "uint16"),
-    "Lf0": sb(72, "float32"), "Lf1": sb(72, "float32"), "Lq": sb(72, "float32"),
-    "La": sb(48, "uint16"), "Lb": sb(48, "uint16"), "SEL": sb(8, "uint16"),
-    "ZL": sb(LC, "uint16"), "ZLf": sb(LC, "float32"), "KL": sb(36, "uint16"),
-    "pi0": sb(1, "int32"), "fi": sb(6, "int32"), "F": sb(6, "float32"), "Cc": sb(80, "float32"),
-    "C16": sb(LC, "float32"), "MT": sb(LC, "float32"), "INC": sb(40, "bfloat16"),
-    "Rx": sb(176, "bfloat16"), "TA": sb(128, "bfloat16"), "TB": sb(128, "bfloat16"), "TC": sb(128, "bfloat16"),
-    "TD": sb(128, "bfloat16"), "SU": sb(8, "bfloat16"),
-    "BP": sb(160, "bfloat16"), "BI": sb(160, "bfloat16"), "BR": sb(144, "bfloat16"), "BL": sb(176, "bfloat16"),
-    "ONES": sb(PIECE, "bfloat16"), "OFFM": sb(128, "bfloat16"),
+    "PM": sb(QUART, "float16"), "PEh": sb(128, "float16"), "X": sb(QUART, "float32"), "RD": sb(QUART, "bfloat16"), "ZR": sb(QUART, "bfloat16"),
+    "IW": sb(Z + 16, "bfloat16"), "W0": sb(Z, "bfloat16"), "ZW": sb(Z, "bfloat16"),
+    "KV": sb(QUART, "bfloat16"), "VAL": sb(QUART, "bfloat16"), "TAB": sb(QUART, "bfloat16"),
+    "Wa": sb(QUART, "bfloat16"), "Wb": sb(QUART, "bfloat16"), "GM": sb(QUART, "bfloat16"), "MK": sb(QUART, "bfloat16"),
+    "DW": sb(QUART, "bfloat16"), "LEN": sb(DUMP + QUART, "bfloat16"), "OFF": sb(QUART, "float32"), "GO": sb(QUART, "float16"),
+    "DAT": sb(Z + HALO, "bfloat16"), "TT": sb(QUART, "bfloat16"), "RR": sb(QUART, "bfloat16"), "XW": sb(Z, "bfloat16"),
+    "OUT": sb(HALF, "bfloat16"), "FL": sb(FIRST + HALO, "bfloat16"),
+    "L": sb(36, "uint16"), "LI": sb(36, "uint16"), "LT": sb(36, "uint16"), "LP": sb(36, "uint16"), "ZO": sb(36, "uint16"),
+    "LTf": sb(36, "float32"), "B1": sb(36, "float32"), "B2": sb(36, "float32"),
+    "La": sb(36, "uint16"), "Lb": sb(36, "uint16"), "ZL": sb(LC, "uint16"), "ZLf": sb(LC, "float32"),
+    "pi0": sb(1, "int32"), "fi": sb(8, "int32"), "F": sb(8, "float32"), "Cc": sb(100, "float32"),
+    "C16": sb(LC, "float32"), "MT": sb(LC, "float32"), "CNT": sb(2, "float32"), "TRI": sb(128, "float32"),
+    "Rx": sb(228, "bfloat16"), "H": sb(PIECE, "bfloat16"), "TB": sb(160, "bfloat16"),
+    "T8": sb(128, "bfloat16"), "VT": sb(8, "bfloat16"), "VS": sb(12, "bfloat16"), "ZT": sb(16, "bfloat16"), "ML": sb(140, "bfloat16"),
+    "ONES": sb(PIECE, "bfloat16"), "OFFM": sb(128, "bfloat16"), "BLo": sb(144, "float16"),
 }
-for _m in ["M1", "MRB", "MA", "MB", "MRG", "NM", "RQ0", "RQ1", "RQ2", "RQ3", "PRE", "PREm", "PRE6",
-           "RP0", "RP1", "R60", "R61", "NEGI"]:
+for _m in ["SR", "MA", "MB", "WW", "WW0", "DG3", "MM", "NEG", "REP"]:
     SCRATCH[_m] = sb(128, "bfloat16")
-for _m in ["EA", "EB"]:
-    SCRATCH[_m] = sb(176, "bfloat16")
-for _m in ["FA", "FB", "PK", "GP0", "GP1"]:
-    SCRATCH[_m] = sb(132, "bfloat16")
+for _m in ["EQ", "EA", "EB"]:
+    SCRATCH[_m] = sb(228, "bfloat16")
+for _m in ["BLh", "BLi", "BLd", "BLk"]:
+    SCRATCH[_m] = sb(144, "bfloat16")
 for _b in range(8):
     SCRATCH["b%d" % _b] = ("psum", [128, 512], "float32")
 
-NDMA = 40
+NDMA = 44
 SEMAPHORES = (["sv", "ss", "sp", "sg", "sent", "hop"] + ["d%d" % i for i in range(NDMA)]
               + ["al%d" % i for i in range(DD)] + ["ax%d" % i for i in range(N)] + ["ay%d" % i for i in range(R)])
 
-CALLS = [[(1, "self", 0), (2, "far", 0), (4, "far", 1)], [(3, "self", 0), (6, "far", 2), (7, "near", 0)], [(5, "self", 0)]]
-ARRIVAL = [1, 3, 5, 2, 4, 7, 6]
+CALLS = [[(1, "self", 0), (2, "far", 0)], [(3, "self", 0), (4, "far", 1)], [(5, "self", 0), (6, "far", 2)], [(7, "near", 0)]]
+ARRIVAL = [1, 3, 2, 5, 4, 6, 7]
+EARLY = 4
+SENDS = [[1, 2, 3], [0, 3, 2], [0, 3, 1], [1, 2, 0]]
+HOLD = 1
 
 
 def bits(engs):
@@ -103,534 +112,586 @@ def rank_program(g, core, T, topo):
         return
     z, h = q // R, q % R
     ops = []
+    V = g.vector
 
-    def add(queue, fn, r=(), w=(), kind="c", sem=None, n=0):
-        ops.append({"q": queue, "fn": fn, "r": list(r), "w": list(w), "kind": kind, "sem": sem, "n": n})
+    def A(name, c0=0, c1=None, step=1, p0=0, p1=128):
+        c1 = SCRATCH[name][1][1] if c1 is None else c1
+        ap = T[name][p0:p1, c0:c1] if step == 1 else T[name][p0:p1, c0:c1:step]
+        return (ap, [(name, p0, p1, c0, c1)])
+
+    def D(ap, name, i=0, n=1):
+        return (ap, [(name, 0, 1, i, i + n)])
+
+    def ind(win, off):
+        return (win[0].indirect(off[0]), win[1], off[1])
+
+    def val(a):
+        return a[0] if isinstance(a, tuple) else a
+
+    def add(queue, fn, out, ins, kind="c", sem=None, n=0):
+        r, w = [], []
+        for a in ins:
+            if isinstance(a, tuple):
+                r += a[1] + (a[2] if len(a) > 2 else [])
+        for a in out:
+            w += a[1]
+            r += a[2] if len(a) > 2 else []
+        ops.append({"q": queue, "fn": fn, "r": r, "w": w, "kind": kind, "sem": sem, "n": n})
 
     ndma = [0]
 
-    def dma(out, in_, r, w, queue="sync"):
+    def dma(out, in_, queue="sync"):
         eng = g.sync if queue == "sync" else g.scalar
-        add(queue, lambda: eng.dma_start(out, in_), r, w, "d", "d%d" % ndma[0], 16)
+        add(queue, lambda: eng.dma_start(out[0], in_[0]), [out], [in_], "d", "d%d" % ndma[0], 16)
         ndma[0] += 1
 
-    def landed(sem, n, key):
-        add(None, None, (), [key], "x", sem, n)
+    def landed(sem, n, reg):
+        add(None, None, [reg], (), "x", sem, n)
 
-    V = g.vector
-
-    def ts(out, in0, s1, s2, o0, o1, r, w):
+    def ts(out, in0, s1, s2=None, o0=Op.add, o1=None):
         if o1 is None:
-            add("v", lambda: V.tensor_scalar(out, in0, s1, None, o0), r, w)
+            add("v", lambda: V.tensor_scalar(out[0], in0[0], val(s1), None, o0), [out], [in0, s1])
         else:
-            add("v", lambda: V.tensor_scalar(out, in0, s1, s2, o0, o1), r, w)
+            add("v", lambda: V.tensor_scalar(out[0], in0[0], val(s1), val(s2), o0, o1), [out], [in0, s1, s2])
 
-    def tt(out, in0, in1, o, r, w):
-        add("v", lambda: V.tensor_tensor(out, in0, in1, o), r, w)
+    def tt(out, in0, in1, o):
+        add("v", lambda: V.tensor_tensor(out[0], in0[0], in1[0], o), [out], [in0, in1])
 
-    def cp(out, in_, r, w):
-        add("v", lambda: V.tensor_copy(out, in_), r, w)
+    def cp(out, in_):
+        add("v", lambda: V.tensor_copy(out[0], in_[0]), [out], [in_])
 
-    def ms(ap, c, w):
-        add("v", lambda: V.memset(ap, c), (), w)
+    def ms(out, c):
+        add("v", lambda: V.memset(out[0], c), [out], ())
 
-    def act(out, in_, r, w, **kw):
-        add("s", lambda: g.scalar.activation(out, in_, Act.Identity, **kw), r, w)
+    def scan(out, d0, d1, init, o1):
+        add("v", lambda: V.tensor_tensor_scan(out[0], d0[0], d1[0], val(init), Op.add, o1), [out], [d0, d1, init])
 
-    def mm(out, lhsT, rhs, start, stop, r, bank):
-        add("p", lambda: g.tensor.matmul(out, lhsT, rhs, start, stop), r, [bank])
+    def act(out, in_, scale=1.0, bias=0.0, func=Act.Identity, acc=None):
+        kw = {} if acc is None else {"accum_out": acc[0]}
+        add("s", lambda: g.scalar.activation(out[0], in_[0], func, bias=val(bias), scale=val(scale), **kw),
+            [out] + ([] if acc is None else [acc]), [in_, scale, bias])
 
-    def iota(out, pattern, base, cm, w, small=True):
+    def mm(out, lhsT, rhs, start, stop):
+        add("p", lambda: g.tensor.matmul(out[0], lhsT[0], rhs[0], start, stop), [out], [lhsT, rhs])
+
+    def iota(out, pattern, base, cm=0, small=True):
         if small:
-            add("g", lambda: g.iota(out, pattern, base, cm, allow_small_or_imprecise_dtypes=True), (), w)
+            add("g", lambda: g.iota(out[0], pattern, base, cm, allow_small_or_imprecise_dtypes=True), [out], ())
         else:
-            add("g", lambda: g.iota(out, pattern, base, cm), (), w)
+            add("g", lambda: g.iota(out[0], pattern, base, cm), [out], ())
 
     sent = [0]
 
-    def remote(transfers, r):
+    def remote(transfers, after=()):
         tr = []
-        for src, dst, c, engs, sem in transfers:
+        for src, dst, c, engs, rsem in transfers:
             rid, pid = topo.addr(c, core)
             tr.append(RemoteDMATransfer(dst_ids=[DstId(rid=rid, pnc=pid)], dma_engine_mask=bits(engs),
-                                        remote_sem=T.sem[sem], src=src, dst=dst))
+                                        remote_sem=T.sem[rsem], src=src[0], dst=dst))
             sent[0] += len(engs)
-        add("g", lambda: g.remote_dma_fused(tr, local_sem=T.sem.sent), r, (), "r")
+        add("g", lambda: g.remote_dma_fused(tr, local_sem=T.sem.sent), [], [t[0] for t in transfers] + list(after), "r")
 
-    B = [T["b%d" % i] for i in range(8)]
-    bk = ["b%d" % i for i in range(8)]
+    def B(b, c0=0, c1=PIECE):
+        return A("b%d" % b, c0, c1)
+
     rows = slice(32 * h, 32 * h + 32)
     off_engs = topo.engines(core, T.cores[(q + 1) % N])
     noff = len(off_engs)
     order = [q] + [(q - k) % N for k in ARRIVAL]
     data = [s for s in order if s < DD]
-    tiles = {"A": order[:4], "B": order[4:]}
-    chunk = lambda c: slice(CH * c, CH * c + CH)
-    piece = lambda c: slice(PIECE * c, PIECE * c + PIECE)
-    j0 = lambda s4: HALF * (s4 % 2) + QUART * (s4 // 2)
+    tiles = {"A": [(q - k) % N for k in range(4)], "B": [(q - k) % N for k in range(4, 8)]}
+
+    def P2(name, e):
+        return A(name, PIECE * e, PIECE * e + PIECE)
+
+    def L2(name, e):
+        return A(name, 18 * e, 18 * e + 18)
+
+    def shift(name, f, p1=128):
+        return A(name, 100 - 32 * f, 228 - 32 * f, p1=p1)
 
     if q < DD:
-        dma(T.PS[0:512, :], T.pi[:, 0:LC], (), ["PS0"], "sync")
-        dma(T.PS[512:1024, :], T.pi[:, LC:2 * LC], (), ["PS1"], "scalar")
-    dma(T.Zi[0:32, :], T.zero[rows, :], (), ["Zi"], "scalar")
-    dma(T.Li[0:32, 0:2], T.lost[rows, :], (), ["Li"], "scalar")
-    steps = send_steps(T, topo, q)
-    for st in steps:
-        for d, c, engs in st:
-            dma(T.XS[128 * d:128 * d + 128, :], T.x[32 * (d % R):32 * (d % R) + 32, Z * (d // R):Z * (d // R) + Z], (), ["XS%d" % d])
-    iota(T.pi0[:], [[0, 1]], 0, 1, ["pi0"], False)
-    iota(T.TA[:], [[16, 2], [0, 4], [1, 16]], 0, 0, ["TA"])
-    iota(T.Rx[:], [[1, 176]], -48, 0, ["Rx"])
-    iota(T.C16[:], [[16, LC]], 0, 0, ["C16"])
-    iota(T.TB[:], [[0, 4], [1, 32]], 0, 0, ["TB"])
-    iota(T.TD[:], [[64, 2], [0, 4], [1, 16]], 0, 0, ["TD"])
-    if q < DD:
-        remote([(T.PS[128 * d:128 * d + 128, :], T.PL[q], T.cores[d], [off_engs[i]], "al%d" % q)
-                for i, d in enumerate([(q + k) % N for k in range(1, N)])], ["PS0", "PS1"])
-    for st in steps:
-        remote([(T.XS[128 * d:128 * d + 128, :], T.XL[q if c == T.cores[d] else 0], c, engs,
-                 "ax%d" % q if c == T.cores[d] else "hop") for d, c, engs in st], ["XS%d" % d for d, c, engs in st])
-    iota(T.TC[:], [[32, 4], [0, 2], [1, 16]], 0, 0, ["TC"])
-    iota(T.SU[:], [[64, 2], [0, 2], [16, 2]], 0, 0, ["SU"])
-    for s in range(N):
-        if s != q:
-            landed("ax%d" % s, noff, "XL%d" % s)
-            if s < DD:
-                landed("al%d" % s, 1, "PL%d" % s)
-    for s in range(R):
-        if s != h:
-            landed("ay%d" % s, noff, "YL%d" % s)
+        dma(D(T.PS[0:512, :], "PS", 0, 4), D(T.pi[:, 0:LC], "pi"), "sync")
+        dma(D(T.PS[512:1024, :], "PS", 4, 4), D(T.pi[:, LC:2 * LC], "pi"), "scalar")
+    dma(A("Zi", p1=32), D(T.zero[rows, :], "zero"), "scalar")
+    dma(A("Li", 0, 2, p1=32), D(T.lost[rows, :], "lost"), "scalar")
 
-    def lists_of(s):
-        return (T.pi[rows, LC * z:LC * z + LC], []) if s == q else (T.PL[s], ["PL%d" % s])
+    def where(s):
+        return "AB"[(q - s) % N // 4], 32 * ((q - s) % 4)
+
+    def lists_to(s):
+        t, p0 = where(s)
+        return A("L%si" % t, p0=p0, p1=p0 + 32)
+
+    def load_list(s):
+        dma(lists_to(s), D(T.pi[rows, LC * z:LC * z + LC], "pi") if s == q else D(T.PL[s], "PL", s))
+
+    def stage(d):
+        dma(D(T.XS[128 * d:128 * d + 128, :], "XS", d),
+            D(T.x[32 * (d % R):32 * (d % R) + 32, Z * (d // R):Z * (d // R) + Z], "x"))
 
     def place(s):
-        src, r = (T.x[rows, Z * z:Z * z + Z], []) if s == q else (T.XL[s], ["XL%d" % s])
-        t, i = "AB"[order.index(s) // 4], order.index(s) % 4
-        dma(T["X" + t][32 * i:32 * i + 32, :], src, r, ["X%s%d" % (t, i)])
+        src = D(T.x[rows, Z * z:Z * z + Z], "x") if s == q else D(T.XL[s], "XL", s)
+        t, p0 = where(s)
+        dma(A("X" + t, p0=p0, p1=p0 + 32), src)
 
-    place(q)
+    for s in range(N):
+        if s != q:
+            landed("ax%d" % s, noff, D(None, "XL", s))
+            if s < DD:
+                landed("al%d" % s, 1, D(None, "PL", s))
+    for s in range(R):
+        if s != h:
+            landed("ay%d" % s, noff, D(None, "YL", s))
+    steps = send_steps(T, topo, q)
+    out_order = [d for st in steps for d, c, engs in st]
+    if q < DD:
+        load_list(q)
+    for d in out_order[:EARLY]:
+        stage(d)
     for s in data:
-        src, r = lists_of(s)
-        dma(T.LS[:, 36 * s:36 * s + 36], src, r, ["LS%d" % s])
-    for s in data:
-        src, r = lists_of(s)
-        t, i = "AB"[order.index(s) // 4], order.index(s) % 4
-        dma(T["L%si" % t][32 * i:32 * i + 32, :], src, r, ["L%si%d" % (t, i)])
-    for s in order[1:]:
+        if s != q:
+            load_list(s)
+    for d in out_order[EARLY:]:
+        stage(d)
+    for s in order:
         place(s)
-    kLS = ["LS%d" % s for s in range(DD)]
-    kX = {t: ["X%s%d" % (t, i) for i in range(4)] for t in "AB"}
+    iota(A("pi0"), [[0, 1]], 0, 1, False)
+    iota(A("TB"), [[0, 5], [1, 32]], 0)
+    step_e, step_f = [[2, 2], [0, 2]], [[0, 2], [-4, 2]]
+    iota(A("VS", 0, 4), step_f, 2)
+    iota(A("VS", 4, 8), step_e, -1)
+    iota(A("VS", 8, 12), step_f, 2)
+    iota(A("VT"), [[0, 4], [1, 2]], 0)
+    iota(A("Rx"), [[1, 228]], 0)
+    iota(A("C16"), [[16, LC]], 0)
+    if q < DD:
+        remote([(D(T.PS[128 * d:128 * d + 128, :], "PS", d), T.PL[q], T.cores[d], [off_engs[i]], "al%d" % q)
+                for i, d in enumerate([(q + k) % N for k in range(1, N)])])
+    iota(A("T8"), [[1, 16], [0, 8]], 0)
+    iota(A("ZT", 0, 1), [[0, 1]], 128)
+    iota(A("ZT", 1, 16), [[0, 15]], -int(OFFSET))
+    for n, st in enumerate(steps):
+        remote([(D(T.XS[128 * d:128 * d + 128, :], "XS", d), T.XL[q if c == T.cores[d] else 0], c, engs,
+                 "ax%d" % q if c == T.cores[d] else "hop") for d, c, engs in st],
+               [lists_to(s) for s in data] if n >= HOLD else [])
+    iota(A("ONES"), [[0, PIECE]], 1)
+    iota(A("OFFM"), [[0, 128]], int(OFFSET) // 32)
+    iota(A("FL"), [[0, FIRST + HALO]], FLOOR)
+    iota(A("LEN", 0, DUMP), [[0, DUMP]], 0)
+    iota(A("DAT"), [[0, Z + HALO]], 0)
 
-    ms(T.ZW[:], 0.0, ["ZW"])
-    fields = {"p": 127, "p32": 31, "r": 15, "u64": 64, "p3": 3, "e16": 16}
-    F = {}
-    for i, name in enumerate(fields):
-        ts(T.fi[:, i:i + 1], T.pi0[:], fields[name], None, Op.bitwise_and, None, ["pi0"], ["fi%d" % i])
-        F[name] = T.F[:, i:i + 1]
-    cp(T.F[:], T.fi[:], ["fi%d" % i for i in range(6)], ["F"])
-    for nm in ["BP", "BI", "BR", "BL"]:
-        ms(T[nm][:], 0.0, [nm])
-    ncol = [0]
+    fields = {"f32": 96, "e16": 16, "p32": 31, "r": 15, "c": 3, "b4": 4}
     C = {}
+    ms(A("ZW", 0, QUART), 0.0)
+    for i, name in enumerate(fields):
+        ts(A("fi", i, i + 1), A("pi0"), fields[name], None, Op.bitwise_and)
+        C[name] = A("F", i, i + 1)
+    ncol = [0]
     at = {}
 
     def slot(name, n=1):
         at[name] = ncol[0]
-        C[name] = T.Cc[:, ncol[0]:ncol[0] + n]
+        C[name] = A("Cc", ncol[0], ncol[0] + n)
         ncol[0] += n
+        return C[name]
 
-    def col(name, in0, s1, s2, o0, o1, r, n=1):
-        slot(name, n)
-        ts(C[name], in0, s1, s2, o0, o1, ["F"] + r, [name])
+    def col(name, in0, s1, s2, o0, o1=None, n=1):
+        ts(slot(name, n), in0, s1, s2, o0, o1)
 
-    def lin(name, in0, scale, bias, r, n=1):
-        slot(name, n)
-        act(C[name], in0, ["F"] + r, [name], scale=scale, bias=bias)
+    def lin(name, in0, scale, bias, n=1):
+        act(slot(name, n), in0, scale, bias)
 
-    def e(name, i):
-        return T.Cc[:, at[name] + i:at[name] + i + 1]
+    def el(name, i):
+        return A("Cc", at[name] + i, at[name] + i + 1)
 
-    def mat(name, table, tkey, code, wgt, r, o1=Op.mult, out=None):
-        ts(T[name][:] if out is None else out, table, code, wgt, Op.is_equal, o1 if wgt is not None else None,
-           ["F", tkey] + r, [name])
+    def mat(out, table, code, wgt=None):
+        ts(out, table, code, wgt, Op.is_equal, None if wgt is None else Op.mult)
 
-    lin("p63", F["u64"], -1.0, F["p"], [])
-    lin("cE", F["e16"], 4.0, F["r"], [])
-    lin("p60", F["p3"], -1.0, C["p63"], ["p63"])
-    lin("p48", F["r"], -1.0, C["p63"], ["p63"])
-    lin("kc0", C["p60"], 0.25, 0.0, ["p60"])
-    lin("k32", F["p32"], -1.0, C["p63"], ["p63"])
-    lin("kc", F["p3"], float(QUART), C["kc0"], ["kc0"])
-    lin("cTC", F["e16"], -1.0, F["p"], [])
-    lin("cTD", F["u64"], 1.0, F["r"], [])
-    lin("p80", F["u64"], 1.0, F["e16"], [])
-    lin("cF", F["p32"], 4.0, 0.0, [])
-    lin("cK", F["r"], 4.0, F["u64"], [])
-    lin("we1", F["e16"], 1.0 / 16.0, 0.0, [])
-    lin("we0", F["e16"], -1.0 / 16.0, 1.0, [])
-    lin("c32", C["cTD"], 1.0, 32.0, ["cTD"])
-    lin("c80", C["p80"], 1.0, 32.0, ["p80"])
-    lin("ck", C["k32"], 1.0 / 32.0, 0.0, ["k32"])
-    lin("cd", C["k32"], -1.0 / 32.0, 1.0, ["k32"])
-    lin("cb", C["k32"], OFFSET / 32.0, 0.0, ["k32"])
-    lin("cG", C["k32"], 1.0 / 16.0, C["cK"], ["k32", "cK"])
-    slot("disk", 2)
-    kD = []
-    for n, t in enumerate("AB"):
-        for i in range(4):
-            ms(T.Cc[32 * i:32 * i + 32, at["disk"] + n:at["disk"] + n + 1], float(tiles[t][i]), ["disk%d" % (4 * n + i)])
-            kD.append("disk%d" % (4 * n + i))
-    col("e5", T.Rx[:, 48:53], F["r"], None, Op.is_equal, None, ["Rx"], 5)
-    mat("M1", T.TA[:], "TA", F["p32"], None, [])
-    col("m01", F["r"], 2.0, None, Op.is_lt, None, [])
-    col("hi", e("e5", 0), e("e5", 3), 4.0, Op.add, Op.mult, ["e5"])
-    col("lo", e("e5", 1), e("e5", 4), None, Op.add, None, ["e5"])
-    col("c256", e("e5", 2), 256.0, None, Op.mult, None, ["e5"])
-    ts(T.MT[:], T.C16[:], F["r"], None, Op.add, None, ["C16", "F"], ["MT"])
-    ts(T.INC[:], T.C16[:, 0:40], C["hi"], None, Op.mult, None, ["C16", "hi"], ["INC"])
-    ts(T.IW[:, 0:64], T.Rx[:, 48:112], C["lo"], C["c256"], Op.mult, Op.add, ["Rx", "lo", "c256"], ["IW"])
-    ts(T.ZB[0:32, 0:LC], T.Zi[0:32, :], float(Z), None, Op.mult, None, ["Zi"], ["ZB0"])
-    cp(T.ZB[0:32, LC:LC + 2], T.Li[0:32, 0:2], ["Li"], ["ZB1"])
-    mm(B[6][:, 0:LC + 2], T.M1[0:32, :], T.ZB[0:32, 0:LC + 2], True, True, ["M1", "ZB0", "ZB1"], bk[6])
-
-    def grow(s):
-        n = 64 << s
-        m = min(n, 2368 - n)
-        ts(T.IW[:, n:n + m], T.IW[:, 0:m], T.INC[:, 1 << s:(1 << s) + 1], None, Op.add, None, ["IW", "INC"], ["IW"])
-
-    grow(0)
-    col("m234", e("e5", 2), e("e5", 3), e("e5", 4), Op.add, Op.add, ["e5"])
-    grow(1)
-    col("wq", T.C16[:, 0:4], C["p48"], None, Op.is_equal, None, ["C16", "p48"], 4)
-    grow(2)
-    tt(T.ZLf[:], T.MT[:], B[6][:, 0:LC], Op.max, ["MT", bk[6]], ["ZLf"])
-    grow(3)
-    ts(T.KL[:], T.C16[:, 0:36], C["kc"], None, Op.add, None, ["C16", "kc"], ["KL"])
-    grow(4)
-    cp(T.ZL[:], T.ZLf[:], ["ZLf"], ["ZL"])
-    grow(5)
-    lin("m34", e("e5", 3), 1.0, e("e5", 4), ["e5"])
-    lin("mptr", C["ck"], C["m01"], 0.0, ["m01", "ck"])
-    lin("nq", C["wq"], -1.0, 0.0, ["wq"], 4)
-    lin("wp0", e("wq", 2), C["m01"], e("wq", 0), ["wq", "m01"])
-    lin("wp1", e("wq", 3), C["m01"], e("wq", 1), ["wq", "m01"])
-    lin("nptr", C["mptr"], -1.0, 0.0, ["mptr"])
-    iw = T.IW[:, 0:2368]
-    act(T.W0[:, HALF:Z], iw.indirect(T.ZL[:, 72:144]), ["IW", "ZL", "m01"], ["W0b"], scale=C["m01"])
-    act(T.KV[:], iw.indirect(T.KL[:]), ["IW", "KL", "m234"], ["KV"], scale=C["m234"])
-    col("ab36", B[6][:, LC:LC + 2], 36.0, None, Op.mult, None, [bk[6]], 2)
-    mat("MRB", T.TB[:], "TB", F["p"], None, [])
-    mm(B[7][:, 0:2], T.MRB[0:32, :], T.ZB[0:32, LC:LC + 2], True, True, ["MRB", "ZB1"], bk[7])
-    ts(T.W0[:, 0:HALF], iw.indirect(T.ZL[:, 0:72]), C["m01"], None, Op.mult, None, ["IW", "ZL", "m01"], ["W0a"])
-    ts(T.SEL[:, 0:3], T.MT[:, 0:3], 35.0, e("ab36", 0), Op.min, Op.add, ["MT", "ab36"], ["SELa"])
-    ts(T.SEL[:, 4:7], T.MT[:, 0:3], 35.0, e("ab36", 1), Op.min, Op.add, ["MT", "ab36"], ["SELb"])
-    col("baseQ", C["disk"], float(DD - 1), float(DD), Op.max, Op.subtract, kD, 2)
-    col("isP", C["disk"], float(DD), 2.0, Op.is_equal, Op.mult, kD, 2)
-    col("isQ", C["disk"], float(DD + 1), 1.0, Op.is_equal, Op.subtract, kD, 2)
-    col("qA", B[7][:, 0:2], e("disk", 0), None, Op.is_equal, None, [bk[7]] + kD, 2)
-    col("qB", B[7][:, 0:2], e("disk", 1), None, Op.is_equal, None, [bk[7]] + kD, 2)
-    slot("baseP", 2)
-    tt(C["baseP"], C["isP"], C["isQ"], Op.add, ["isP", "isQ"], ["baseP"])
-    mat("BP", T.TD[:, 0:128:32], "TD", F["u64"], C["m01"], ["m01", "BP"], out=T.BP[:, 31:128:32])
-    mat("BI", T.TD[:, 0:128:32], "TD", F["u64"], C["m34"], ["m34", "BI"], out=T.BI[:, 31:128:32])
-    for n, t in enumerate("AB"):
-        col("wQ" + t, e("q" + t, 0), e("q" + t, 1), e("baseQ", n), Op.add, Op.add, ["q" + t, "baseQ"])
-        col("wP" + t, e("q" + t, 0), e("q" + t, 1), e("baseP", n), Op.add, Op.add, ["q" + t, "baseP"])
+    cp(A("F", 0, len(fields)), A("fi", 0, len(fields)))
+    ms(A("ZW", QUART, HALF), 0.0)
+    lin("tgt", C["f32"], 1.0 / 32.0, C["e16"])
+    lin("cEQ", C["p32"], 1.0, 100.0)
+    slot("disk0", 2)
+    for n in range(2):
+        act(el("disk0", n), C["f32"], -1.0 / 32.0, float(q - 4 * n))
+    act(A("VT", p0=32, p1=64), A("VS", 4, 12, p0=32, p1=64))
+    act(A("VT", p0=64, p1=96), A("VS", 0, 8, p0=64, p1=96))
+    act(A("VT", p0=96), A("VS", 0, 8, p0=96), 0.0, 1.0)
+    mat(A("SR"), A("TB", 0, 128), C["tgt"], 1.0 / 16.0)
+    col("wrap", C["disk0"], 0.0, float(N), Op.is_lt, Op.mult, n=2)
+    mm(B(4, 0, 8), A("SR"), A("VT"), True, True)
+    act(A("H", 0, 224), A("Rx", 0, 224), 1.0, -144.0)
+    act(A("H", 224, PIECE), A("Rx", 0, 64), 1.0, 80.0)
+    tt(slot("disk", 2), C["disk0"], C["wrap"], Op.add)
+    col("o", A("Rx", 0, 16), C["r"], None, Op.is_equal, n=16)
+    mat(A("EQ"), A("Rx"), C["cEQ"])
+    cp(slot("cb", 8), B(4, 0, 8))
+    col("flag", el("o", 4), el("o", 5), el("o", 6), Op.add, Op.add)
+    lin("k0", C["f32"], 18.0, 144.0)
+    ts(A("ZB", 0, LC, p1=32), A("Zi", p1=32), float(Z), None, Op.mult)
+    ts(A("MT"), A("C16"), C["r"])
+    cp(A("ZB", LC, LC + 2, p1=32), A("Li", 0, 2, p1=32))
+    for f in range(4):
+        mm(B(5, 0, LC + 2), shift("EQ", f, 32), A("ZB", 0, LC + 2, p1=32), f == 0, f == 3)
+    for b in range(8):
+        e, f = b // 4, b % 4
+        cb = el("cb", 4 * (f // 2) + 2 * e + f % 2)
+        blk = A("IW", PIECE * b, PIECE * b + PIECE)
+        if b < 5:
+            ts(blk, A("H"), el("o", 0), cb, Op.mult, Op.add)
+        else:
+            act(blk, A("H"), el("o", 0), cb)
+    act(A("IW", Z, Z + 16), A("Rx", 0, 16), 0.0, C["flag"])
+    tt(A("ZLf"), A("MT"), B(5, 0, LC), Op.max)
+    col("qA", B(5, LC, LC + 2), el("disk", 0), None, Op.is_equal, n=2)
+    col("qB", B(5, LC, LC + 2), el("disk", 1), None, Op.is_equal, n=2)
+    cp(A("ZL"), A("ZLf"))
+    lin("kc0", C["k0"], el("o", 15), 0.0)
+    lin("rest0", C["flag"], -1.0, 1.0)
+    cut = 1440
+    act(A("W0", Z - cut, Z), ind(A("IW"), A("ZL", (Z - cut) // 16, LC)))
+    for t in "AB":
         for i, s in enumerate(tiles[t]):
             if s >= DD:
-                cp(T["L%si" % t][32 * i:32 * i + 32, :], T.MT[32 * i:32 * i + 32, :], ["MT"], ["L%si%d" % (t, i)])
-    f131 = T.Rx[:, 45:176]
-    diag = T.Rx[:, 48:176]
+                cp(lists_to(s), A("MT", p0=32 * i, p1=32 * i + 32))
+    for n, ab in enumerate("ab"):
+        for t in "AB":
+            mat(A("S" + ab + t), A("Rx"), C["cEQ"], el("q" + t, n))
+    cp(A("W0", 0, Z - cut), ind(A("IW"), A("ZL", 0, (Z - cut) // 16)))
+    ms(A("ZW", HALF, Z), 0.0)
+    for e in range(2):
+        for f in range(4):
+            mm(B(e), A("EQ", 96 - 32 * f, 224 - 32 * f, p1=32), A("IW", HALF * e + PIECE * f, HALF * e + PIECE * f + PIECE, p1=32),
+               f == 0, f == 3)
+    for e in range(2):
+        for f in range(4):
+            mm(B(2, 18 * e, 18 * e + 18), shift("EQ", f, 32), A("ZB", 72 * e + 18 * f, 72 * e + 18 * f + 18, p1=32), f == 0, f == 3)
+    lin("kc1", el("o", 15), float(PIECE), C["kc0"])
+    lin("rest", el("o", 7), -1.0, C["rest0"])
+    for e in range(2):
+        act(P2("KV", e), A("H"), el("o", 11), C["kc%d" % e])
+    for e in range(2):
+        act(P2("TAB", e), B(e), C["flag"], C["rest"])
+    col("oc", A("Rx", 0, 4), C["c"], None, Op.is_equal, n=4)
+    col("lo8", C["r"], 8.0, None, Op.is_lt)
+    lin("s16", C["f32"], 1.0, C["e16"])
+    lin("cW0", C["f32"], 0.125, C["e16"])
+    lin("xy", el("oc", 1), 1.0, el("oc", 2))
+    lin("wh0", el("oc", 0), 2.0, 0.0)
+    lin("wk0", C["lo8"], -1.0, 1.0)
+    lin("p", C["f32"], 1.0, C["p32"])
+    lin("sg", C["b4"], -0.5, 1.0)
+    lin("cW", C["c"], 1.0, C["cW0"])
+    lin("cBL", C["s16"], 1.0, 15.0)
+    lin("cM", C["s16"], 0.125, el("oc", 1))
+    lin("wh", C["xy"], 0.5, C["wh0"])
+    lin("wk", C["wk0"], el("oc", 3), 0.0)
+
     for t in "AB":
-        mat("E" + t, T.Rx[:], "Rx", C["cE"], C["wP" + t], ["wP" + t, "cE"])
-        mat("M" + t, T.TA[:], "TA", F["p32"], C["wQ" + t], ["wQ" + t])
+        ts(A("L%sh" % t), A("L%si" % t), -float(HALF))
+    for n, ab in enumerate("ab"):
+        for t in "AB":
+            for f in range(4):
+                mm(B(4 + n, 0, 36), shift("S" + ab + t, f), A("L%sh" % t, 36 * f, 36 * f + 36), t == "A" and f == 0, t == "B" and f == 3)
+    ts(A("ZO"), B(2, 0, 36), 1.0, None, Op.min)
+    col("cd1", C["f32"], 0.125, 3.0, Op.mult, Op.add)
+    ts(A("La"), B(4, 0, 36), float(HALF))
+    ts(A("Lb"), B(5, 0, 36), float(HALF))
+    cp(P2("VAL", 0), ind(A("W0"), L2("La", 0)))
+    act(P2("VAL", 1), ind(A("W0"), L2("La", 1)))
+    ts(A("B1"), B(2, 0, 36), -4.0, float(DUMP - K2), Op.mult, Op.add)
+    tt(ind(A("ZW"), A("Lb")), A("VAL"), A("KV"), Op.add)
+    thirds = [(0, 0, PIECE), (1, 0, 160), (1, 160, PIECE)]
+    for n, (e, c0, c1) in enumerate(thirds):
+        for f in range(4):
+            a = HALF * e + PIECE * f
+            mm(B(5 + n, 0, c1 - c0), shift("EQ", f), A("ZW", a + c0, a + c1), f == 0, f == 3)
+    mat(A("WW0"), A("TB", 0, 128), C["cW"], C["lo8"])
+    mat(A("MM"), A("T8"), C["cM"], C["xy"])
+    mat(A("BLh"), A("Rx", 0, 144), C["cBL"], C["wh"])
+    mat(A("WW"), A("TB", 0, 128), C["cW"])
+    mat(A("DG3"), A("Rx", 0, 128), C["p"], el("oc", 3))
+    mat(A("BLk"), A("Rx", 0, 144), C["cBL"], C["wk"])
 
-    cp(T.La[:], T.LS[:].indirect(T.SEL[:, 0:3]), kLS + ["SELa"], ["La"])
-    cp(T.Lb[:], T.LS[:].indirect(T.SEL[:, 4:7]), kLS + ["SELb"], ["Lb"])
-    act(T.VAL[:, piece(1)], T.W0[:].indirect(T.La[:, 18:36]), ["W0a", "W0b", "La"], ["VAL1"])
-    cp(T.VAL[:, piece(0)], T.W0[:].indirect(T.La[:, 0:18]), ["W0a", "W0b", "La"], ["VAL0"])
-    cp(T.LA[:], T.LAi[:], ["LAi%d" % i for i in range(4)], ["LA"])
-    cp(T.LB[:], T.LBi[:], ["LBi%d" % i for i in range(4)], ["LB"])
-    tt(T.ZW[:].indirect(T.Lb[:, 0:36]), T.VAL[:], T.KV[:], Op.add, ["VAL0", "VAL1", "KV", "Lb", "ZW"], ["ZW"])
+    def to_list(table, src, out, start=True, stop=True, c0=0, c1=QUART):
+        for rho in range(16):
+            mm(out, A(table, 15 - rho, 143 - rho), A(src, c0 + rho, c1, 16), start and rho == 0, stop and rho == 15)
 
-    def half_lists(nm, b):
-        for eta in range(2):
-            for rho in range(16):
-                x0 = 15 - rho + 16 - 16 * eta
-                mm(B[b][:, CH:CH + 72], T[nm][:, x0:x0 + 128], T.ZW[:, HALF * eta + rho:HALF * eta + HALF:16],
-                   eta == 0 and rho == 0, eta == 1 and rho == 15, [nm, "ZW"], bk[b])
+    lin("wi0", el("oc", 1), U / 2.0, el("oc", 0))
+    lin("noc", el("oc", 0), -1.0, 0.0)
+    lin("su", C["e16"], 0.125, -1.0)
+    lin("th0", C["e16"], 3.0 / 16.0, 1000.0)
+    lin("cP0", C["f32"], 1.0 / 32.0, 0.0)
+    lin("wi", el("oc", 2), 5.0 * U / 2.0, C["wi0"])
+    lin("th1", C["p32"], C["su"], C["th0"])
+    lin("cP", C["p32"], 4.0, C["cP0"])
+    lin("th", el("oc", 0), -1000.0, C["th1"])
+    act(slot("over5", 2), C["disk"], 1.0, -float(DD - 1), Act.Relu)
+    act(slot("over6", 2), C["disk"], 3.0, -3.0 * DD, Act.Relu)
+    for n, t in enumerate("AB"):
+        lin("gone" + t, el("q" + t, 0), 1.0, el("q" + t, 1))
+    for n, t in enumerate("AB"):
+        lin("wQ0" + t, el("over5", n), 1.0, C["gone" + t])
+        lin("wP0" + t, el("over6", n), -1.0, C["gone" + t])
+    for n, t in enumerate("AB"):
+        lin("wQ" + t, C["wQ0" + t], 1.0, -1.0)
+        lin("wP1" + t, el("over5", n), 2.0, C["wP0" + t])
+    for n, t in enumerate("AB"):
+        lin("wP" + t, C["wP1" + t], 1.0, -1.0)
+    col("wd", C["r"], C["cd1"], None, Op.is_equal)
+    tt(A("B2"), A("B1"), A("MT", 0, 36), Op.add)
 
-    def p_quarter(t):
-        for c in range(2):
-            for s4 in range(4):
-                a = j0(s4) + PIECE * c
-                mm(B[6 + c][:, 0:PIECE], T["E" + t][:, 48 - 16 * s4:176 - 16 * s4], T["X" + t][:, a:a + PIECE],
-                   t == "A" and s4 == 0, t == "B" and s4 == 3, kX[t] + ["E" + t], bk[6 + c])
+    def sum_tables():
+        for t in "AB":
+            cp(A("L" + t), A("L%si" % t))
+            mat(A("M" + t), A("TB", 0, 128), C["p32"], C["wQ" + t])
+            mat(A("E" + t), A("Rx"), C["cEQ"], C["wP" + t])
 
-    def p_final(t):
-        for eta in range(2):
-            for t4 in range(4):
-                a = HALF * eta + PIECE * t4
-                mm(B[6 + eta][:, 0:PIECE], T["F" + t][:, 3 - t4:131 - t4], T["X" + t][:, a:a + PIECE], False, False,
-                   kX[t] + ["F" + t], bk[6 + eta])
+    def inverse():
+        cp(A("LI"), B(5, 0, 36))
 
-    half_lists("BI", 5)
-    p_quarter("A")
-    cut = 960
-    act(T.GA[:, cut:Z], T.XA[:].indirect(T.LA[:, cut // 16:LC]), kX["A"] + ["LA"], ["GA1"])
-    cp(T.GA[:, 0:cut], T.XA[:].indirect(T.LA[:, 0:cut // 16]), kX["A"] + ["LA"], ["GA0"])
-    ts(T.Lq[:, 0:36], B[5][:, CH:CH + 36], C["cd"], None, Op.mult, None, [bk[5], "cd"], ["Lq0"])
-    ts(T.Lq[:, 36:72], B[5][:, CH + 36:CH + 72], C["ck"], None, Op.mult, None, [bk[5], "ck"], ["Lq1"])
-    col("m012", F["r"], 3.0, None, Op.is_lt, None, [])
-    tt(T.Lf1[:, 0:36], T.Lq[:, 0:36], T.Lq[:, 36:72], Op.add, ["Lq0", "Lq1"], ["Lf1"])
-    col("c34", F["p"], 34.0, OFFSET / 256.0, Op.is_equal, Op.mult, [])
-    mat("NM", diag, "Rx", F["p"], C["nptr"], ["nptr"])
-    cp(T.LI[:], T.Lf1[:, 0:36], ["Lf1"], ["LI"])
-    mat("MRG", T.TC[:], "TC", C["c32"], C["m012"], ["c32", "m012"])
-    for s4 in range(4):
-        mat("RQ%d" % s4, T.TC[:], "TC", C["cTD"], e("nq", s4), ["nq", "cTD"])
-    for c in range(6):
-        mm(B[c][:, 0:CH], T.MA[:], T.GA[:, chunk(c)], True, False,
-           ["MA"] + [["GA0"], ["GA0"], ["GA0", "GA1"], ["GA1"], ["GA1"], ["GA1"]][c], bk[c])
-    p_quarter("B")
-    for c in range(3):
-        act(T.GB[:, chunk(c + 3)], T.XB[:].indirect(T.LB[:, 24 * c + 72:24 * c + 96]), kX["B"] + ["LB"], ["GB%d" % (c + 3)])
-        cp(T.GB[:, chunk(c)], T.XB[:].indirect(T.LB[:, 24 * c:24 * c + 24]), kX["B"] + ["LB"], ["GB%d" % c])
-        for cc in [c, c + 3]:
-            mm(B[cc][:, 0:CH], T.MB[:], T.GB[:, chunk(cc)], False, True, ["MB", "GB%d" % cc], bk[cc])
-    for c in range(3):
-        cp(T.QW[:, chunk(c)], B[c][:, 0:CH], [bk[c]], ["QW%d" % c])
-        act(T.QW[:, chunk(c + 3)], B[c + 3][:, 0:CH], [bk[c + 3]], ["QW%d" % (c + 3)])
-    cp(T.PQ[:, piece(0)], B[6][:, 0:PIECE], [bk[6]], ["PQ0"])
-    act(T.PQ[:, piece(1)], B[7][:, 0:PIECE], [bk[7]], ["PQ1"])
-    kQW = ["QW%d" % c for c in range(6)]
-    for nm in ["Wa", "Wb", "W6"]:
-        act(T[nm][:, Z:Z + 16], T.TA[:, 0:16], ["TA"], [nm + "s"], scale=0.0)
-    act(T.ONES[0:32, :], T.IW[0:32, 0:PIECE], ["IW"], ["ONES"], scale=0.0, bias=1.0)
-    act(T.OFFM[0:32, :], T.TA[0:32, :], ["TA"], ["OFFM"], scale=0.0, bias=OFFSET / 32.0)
+    def order_tables():
+        mat(A("BLi"), A("Rx", 0, 144), C["cBL"], C["wi"])
+        mat(A("BLo"), A("Rx", 0, 144), C["cBL"], C["noc"])
+        mat(A("BLd"), A("Rx", 0, 144), C["cBL"], C["wd"])
+        mat(A("ML"), A("TB", 20, 160), C["e16"], C["wd"])
+        ts(A("TRI"), A("TB", 0, 128), C["su"], C["th"], Op.mult, Op.is_gt)
 
-    def parts(c):
-        a = CH * (c % 3)
-        return [(a, a + CH)] if c % 3 != 1 else [(a, QUART), (QUART, a + CH)]
+    def end_tables():
+        mat(A("PEh"), A("Rx", 0, 128), C["cP"])
+        mat(A("NEG"), A("Rx", 0, 128), C["cP"], -1.0)
+        mat(A("REP"), A("TB", 0, 128), C["p32"])
 
-    def pointers(c, lo, hi):
-        a, j = CH * (c % 3), HALF * (c // 3)
-        mm(B[c][:, lo - a:hi - a], T.MRG[:], T.ZW[:, j + lo:j + hi], True, False, ["MRG", "ZW"], bk[c])
-        mm(B[c][:, lo - a:hi - a], T.NM[:], T.IW[:, j + lo:j + hi], False, False, ["NM", "IW"], bk[c])
+    turned = [0]
 
-    half_lists("BP", 2)
-    for c in [0, 3, 2, 5, 1, 4]:
-        pointers(c, *parts(c)[0])
-    for c in range(2):
-        tt(T.X[:, piece(c)], T.QW[:].indirect(T.LI[:, 18 * c:18 * c + 18]), T.PQ[:, piece(c)], Op.subtract,
-           kQW + ["LI", "PQ%d" % c], ["X%d" % c])
-    for c in range(2):
-        ts(B[6 + c][:, 0:PIECE], T.X[:, piece(c)], MAGIC, MAGIC, Op.add, Op.subtract, ["X%d" % c], [bk[6 + c]])
-    for c in range(2):
-        tt(T.RD[:, piece(c)], T.X[:, piece(c)], B[6 + c][:, 0:PIECE], Op.subtract, ["X%d" % c, bk[6 + c]], ["RD%d" % c])
-    mat("PRE", diag, "Rx", F["p"], None, [])
-    mat("RP0", T.TC[:], "TC", C["cTC"], C["wp0"], ["wp0", "cTC"])
-    mat("RP1", T.TC[:], "TC", C["cTC"], C["wp1"], ["wp1", "cTC"])
-    for c in [0, 3, 2, 5, 1, 4]:
-        eta, a = c // 3, CH * (c % 3)
-        for i, (lo, hi) in enumerate(parts(c)):
-            kap = lo // QUART
-            if i:
-                pointers(c, lo, hi)
-            nm = "RQ%d" % (2 * kap + eta)
-            mm(B[c][:, lo - a:hi - a], T[nm][:], T.RD[:, lo - QUART * kap:hi - QUART * kap], False, True, [nm, "RD0", "RD1"], bk[c])
-    for eta in range(2):
-        mm(B[6 + eta][:, 0:PIECE], T.OFFM[0:32, :], T.ONES[0:32, :], True, False, ["OFFM", "ONES"], bk[6 + eta])
-    for c in [0, 2, 1]:
-        if c == 1:
-            cp(T.L0[:], B[2][:, CH:CH + 72], [bk[2]], ["L0"])
-            cp(T.Lf0[:], B[2][:, CH:CH + 72], [bk[2]], ["Lf0"])
-            mat("BR", T.SU[:], "SU", C["p80"], C["mptr"], ["mptr", "BR", "p80"], out=T.BR[:, 15:128:16])
-            act(T.PREm[:], T.PRE[:], ["PRE", "c34"], ["PREm"], bias=C["c34"])
-        cp(T.Wa[:, chunk(c)], B[c][:, 0:CH], [bk[c]], ["Wa%d" % c])
-        act(T.Wa[:, chunk(c + 3)], B[c + 3][:, 0:CH], [bk[c + 3]], ["Wa%d" % (c + 3)])
+    def turn(fn, n):
+        while n:
+            t, a = "AB"[turned[0] // Z], turned[0] % Z
+            m = min(n, Z - a)
+            fn(A("G" + t, a, a + m), ind(A("X" + t), A("L" + t, a // 16, (a + m) // 16)))
+            turned[0] += m
+            n -= m
 
-    def spare(rd):
-        if rd == 1:
-            mat("FA", f131, "Rx", C["cF"], C["wPA"], ["cF", "wPA"], out=T.FA[:, 0:131])
-            mat("FB", f131, "Rx", C["cF"], C["wPB"], ["cF", "wPB"], out=T.FB[:, 0:131])
-            mat("GP0", T.Rx[:, 47:176], "Rx", C["cG"], C["we0"], ["cG", "we0"], out=T.GP0[:, 0:129])
-            act(T.NEGI[:], T.PRE[:], ["PRE"], ["NEGI"], scale=-1.0)
-        if rd == 3:
-            mat("PRE6", T.TD[:], "TD", F["p"], C["c34"], ["c34"], o1=Op.add)
-            mat("R60", T.TD[:], "TD", C["cTD"], e("wq", 0), ["wq", "cTD"])
-            mat("R61", T.TD[:], "TD", C["cTD"], e("wq", 1), ["wq", "cTD"])
-        if rd == 5:
-            mat("BL", T.C16[:, 0:11], "C16", C["c80"], C["mptr"], ["c80", "mptr", "BL"], out=T.BL[:, 15:176:16])
-            mat("PK", f131, "Rx", C["cK"], e("wq", 0), ["cK", "wq"], out=T.PK[:, 0:131])
-            mat("GP1", T.Rx[:, 47:176], "Rx", C["cG"], C["we1"], ["cG", "we1"], out=T.GP1[:, 0:129])
+    QCH = [(0, 512, 7), (512, 960, 5), (960, 1408, 6), (1408, 1856, 7), (1856, Z, 5)]
+    sums = []
+    for t in "AB":
+        for e in range(2):
+            for f in range(4):
+                a = HALF * e + PIECE * f
+                sums.append((B(5 + e), shift("E" + t, f), A("X" + t, a, a + PIECE), t == "A" and f == 0, t == "B" and f == 3))
 
-    names = ["Wa", "Wb", "Wa", "Wb", "Wa", "Wb", "W6"]
-    for rd in range(1, 7):
-        wn, nn = names[rd - 1], names[rd]
-        W, Wn = T[wn], T[nn]
-        ln, lnn = "L%d" % ((rd - 1) % 2), "L%d" % (rd % 2)
-        lf, lfn = "Lf%d" % ((rd - 1) % 2), "Lf%d" % (rd % 2)
-        kW = [wn + str(c) for c in range(6)] + [wn + "s", ln]
-        for c in range(3):
-            a = CH * c
-            if c < 2 or rd % 2:
-                act(T.G[:, a + CH // 2:a + CH], W[:].indirect(T[ln][:, 24 * c + 12:24 * c + 24]), kW, ["G%db" % c])
-                cp(T.G[:, a:a + CH // 2], W[:].indirect(T[ln][:, 24 * c:24 * c + 12]), kW, ["G%da" % c])
-            else:
-                cp(T.G[:, a:a + CH], W[:].indirect(T[ln][:, 24 * c:24 * c + 24]), kW, ["G2a", "G2b"])
-        kG = [["G%da" % c, "G%db" % c] for c in range(3)]
-        allG = kG[0] + kG[1] + kG[2]
-        pre = "PRE6" if rd == 6 else "PREm" if rd % 2 == 0 else "PRE"
-        rep = "R6" if rd == 6 else "RP"
-        own = lambda c: rd % 2 == 0 or c >= 3
+    def p_sums(n):
+        for i in range(n):
+            mm(*sums.pop(0))
 
-        def old(c):
-            if own(c):
-                mm(B[c][:, 0:CH], T[pre][:], W[:, chunk(c)], True, False, [pre, wn + str(c)], bk[c])
+    def p_out(e):
+        cp(P2("PM", e), B(5 + e))
 
-        def new(c):
-            nm = rep + str(c // 3)
-            mm(B[c][:, 0:CH], T[nm][:], T.G[:, chunk(c % 3)], not own(c), True, [nm] + kG[c % 3], bk[c])
+    def q_sums(c):
+        a, b, bank = QCH[c]
+        for t in "AB":
+            mm(B(bank, 0, b - a), A("M" + t), A("G" + t, a, b), t == "A", t == "B")
 
-        lb = 2 * (rd % 2)
-
-        def convert():
-            if rd < 6:
-                for rho in range(16):
-                    mm(B[lb][:, CH:CH + 72], T.BR[:, 15 - rho:143 - rho], T.G[:, rho:HALF:16], rho == 0, rho == 15,
-                       ["BR"] + allG, bk[lb])
-            else:
-                for kap in range(2):
-                    for rho in range(16):
-                        x0 = 15 - rho + 32 - 32 * kap
-                        mm(B[0][:, CH:CH + 36], T.BL[:, x0:x0 + 128], T.G[:, QUART * kap + rho:QUART * kap + QUART:16],
-                           kap == 0 and rho == 0, kap == 1 and rho == 15, ["BL"] + allG, bk[0])
-
-        def take_list():
-            if rd < 6:
-                tt(T[lfn][:], B[lb][:, CH:CH + 72], T[lf][:], Op.add, [bk[lb], lf], [lfn])
-            else:
-                tt(T.Lf0[:, 0:36], B[0][:, CH:CH + 36], T.Lf0[:, 36:72], Op.add, [bk[0], "Lf0"], ["Lf7"])
-
-        def narrow_list():
-            if rd < 6:
-                cp(T[lnn][:], T[lfn][:], [lfn], [lnn])
-            else:
-                cp(T.L7[:], T.Lf0[:, 0:36], ["Lf7"], ["L7"])
-
-        if rd % 2:
-            for c in [3, 4, 5]:
-                old(c)
-            for c in [0, 3, 1, 4]:
-                new(c)
-            convert()
-            new(2)
-            new(5)
-            for c in range(3):
-                if c == 2:
-                    spare(rd)
-                    take_list()
-                tt(Wn[:, chunk(c)], B[c][:, 0:CH], W[:, chunk(c)], Op.add, [bk[c], wn + str(c)], [nn + str(c)])
-                act(Wn[:, chunk(c + 3)], B[c + 3][:, 0:CH], [bk[c + 3]], [nn + str(c + 3)])
-            narrow_list()
+    def q_out(c, queue="s"):
+        a, b, bank = QCH[c]
+        if queue == "s":
+            act(A("QW", a, b), B(bank, 0, b - a), 1.0, 128.0)
         else:
-            for c in range(3):
-                old(c)
-                old(c + 3)
-                new(c)
-                new(c + 3)
-            for i, c in enumerate([0, 3, 1, 4, 2, 5]):
-                if rd < 6:
-                    act(T.TT[:, chunk(c)], B[c][:, 0:CH], [bk[c], "cd", "cb"], ["TT%d" % c], scale=C["cd"], bias=C["cb"])
-                else:
-                    act(T.TT[:, chunk(c)], B[c][:, 0:CH], [bk[c]], ["TT%d" % c])
-                tt(Wn[:, chunk(c)], B[c][:, 0:CH], T.TT[:, chunk(c)], Op.subtract, [bk[c], "TT%d" % c], [nn + str(c)])
-                if i == 0:
-                    convert()
-                    if rd < 6:
-                        p_final("AB"[rd // 2 - 1])
-                if i == 1 and rd == 6:
-                    act(T.Lq[:, 0:36], T.Lf1[:, 0:36], ["Lf1", "cd"], ["Lq0"], scale=C["cd"])
-                    act(T.Lq[:, 36:72], T.Lf1[:, 36:72], ["Lf1", "ck"], ["Lq1"], scale=C["ck"])
-                if i == 2 and rd == 6:
-                    tt(T.Lf0[:, 36:72], T.Lq[:, 0:36], T.Lq[:, 36:72], Op.add, ["Lq0", "Lq1"], ["Lf0"])
-                if i == 3:
-                    take_list()
-                if i == 4:
-                    narrow_list()
+            ts(A("QW", a, b), B(bank, 0, b - a), 128.0)
 
-    kW = ["W6%d" % c for c in range(6)]
-    bank = [3, 1, 6, 7]
-    for eta in range(2):
-        mm(B[bank[eta]][:, 0:PIECE], T.OFFM[0:32, :], T.ONES[0:32, :], True, False, ["OFFM", "ONES"], bk[bank[eta]])
-    act(T.G7[:, piece(1)], T.W6[:].indirect(T.L7[:, 18:36]), kW + ["W6s", "L7"], ["G71"])
-    cp(T.G7[:, piece(0)], T.W6[:].indirect(T.L7[:, 0:18]), kW + ["W6s", "L7"], ["G70"])
-    for t4 in range(4):
-        for eta in range(2):
-            a = HALF * eta + PIECE * t4
-            mm(B[bank[eta]][:, 0:PIECE], T.PK[:, 3 - t4:131 - t4], T.W6[:, a:a + PIECE], False, False,
-               kW[a // CH:(a + PIECE - 1) // CH + 1] + ["PK"], bk[bank[eta]])
-    for eta in range(2):
-        for eps in range(2):
-            mm(B[bank[eta]][:, 0:PIECE], T["GP%d" % eta][:, 1 - eps:129 - eps], T.G7[:, piece(eps)],
-               False, eps == 1, ["GP%d" % eta, "G7%d" % eps], bk[bank[eta]])
-    for s in range(R):
-        b = bank[s]
-        act(T.TT[:, piece(s)], B[b][:, 0:PIECE], [bk[b]], ["TT0", "TT1", "TT2", "TF%d" % s], bias=-127.5)
-        tt(T.OUT[:, piece(s)], B[b][:, 0:PIECE], T.TT[:, piece(s)], Op.subtract, [bk[b], "TF%d" % s], ["OUT%d" % s])
-        if s < 2:
-            mm(B[6 + s][:, 0:PIECE], T.NEGI[:], T.OUT[:, piece(s)], False, True, ["NEGI", "OUT%d" % s], bk[6 + s])
-        if s == h:
-            dma(T.y[rows, :], T.OUT[:, piece(s)], ["OUT%d" % s], ["y%d" % s])
+    def d_gather(e):
+        tt(P2("X", e), ind(A("QW"), L2("LI", e)), P2("PM", e), Op.subtract)
+
+    def d_round(e):
+        act(B(5 + e), P2("X", e), 1.0, MAGIC)
+        act(B(5 + e), B(5 + e), 1.0, -MAGIC)
+
+    def d_cut(e):
+        tt(P2("RD", e), B(5 + e), P2("X", e), Op.subtract)
+
+    VFILL = {0: [(sum_tables,)], 1: [(inverse,), (order_tables,)], 2: [(turn, cp, 512)], 3: [(turn, cp, 512)],
+             4: [(turn, cp, 512)], 5: [(turn, cp, 512)], 6: [(turn, cp, 192), (p_out, 0), (p_out, 1)],
+             7: [(q_out, 0, "v"), (end_tables,)]}
+    SFILL = {0: [(act, A("ZR"), ind(A("ZT"), A("ZO")))], 1: [(turn, act, 448)], 2: [(turn, act, 416)], 3: [(turn, act, 416)], 4: [(turn, act, 416)], 5: [(turn, act, 416)],
+             6: [(turn, act, 256)]}
+    PLATE = {2: [(p_sums, 3)], 3: [(p_sums, 3)], 4: [(p_sums, 3)], 5: [(p_sums, 3)], 6: [(q_sums, 0)]}
+    PEARLY = {3: [(p_sums, 1)], 4: [(p_sums, 1)], 5: [(p_sums, 1)], 6: [(p_sums, 1)],
+              7: [(q_sums, 1), (q_out, 1)]}
+
+    def fill(table, rd):
+        for job in table.get(rd, []):
+            job[0](*job[1:])
+
+    for rd in range(ROUNDS + 1):
+        W, Wn = "W" + "ba"[rd % 2], "W" + "ab"[rd % 2]
+        GM = "GM" if rd else "VAL"
+        last = rd == ROUNDS
+
+        def gather(e):
+            if rd == 0:
+                for n, (half, c0, c1) in enumerate(thirds):
+                    if half == e:
+                        tt(A(GM, PIECE * e + c0, PIECE * e + c1), B(5 + n, 0, c1 - c0), A("TAB", PIECE * e + c0, PIECE * e + c1), Op.mult)
+            else:
+                tt(P2(GM, e), ind(A(W), L2("L", e)), P2("MK", e), Op.mult)
+
+        def window(e):
+            mm(B(e), A("WW" if rd else "WW0"), P2(GM, e), rd == 0, True)
+            if last:
+                act(P2("DW", e), B(e), 1.0, 1.0)
+            else:
+                act(A(Wn, e, QUART, 2), B(e))
+
+        def mask(e):
+            mm(B(2 + e), A("MM"), P2(GM, e), True, True)
+            act(P2("MK", e), B(2 + e), C["sg"], -1.0, Act.Relu, A("CNT", e, e + 1) if last else None)
+
+        gather(0)
+        gather(1)
+        window(0)
+        mask(0)
+        fill(PEARLY, rd)
+        fill(VFILL, rd)
+        if last:
+            to_list("BLi", GM, B(4, 64, 100))
+            window(1)
+            tt(A("LTf"), B(4, 64, 100), A("B2"), Op.max)
+            ts(A("LT"), A("LTf"), float(K2))
+            mask(1)
         else:
-            remote([(T.OUT[:, piece(s)], T.YL[h], T.cores[R * z + s], off_engs, "ay%d" % h)], ["OUT%d" % s])
-    for s in range(R):
-        if s != h:
-            dma(T.y[32 * s:32 * s + 32, :], T.YL[s], ["YL%d" % s], ["y%d" % s], "scalar" if (s - h) % R == 2 else "sync")
+            window(1)
+            to_list("BLh", GM, B(4, 0, 36))
+            ts(A("L"), B(4, 0, 36), 287.5)
+            mask(1)
+            fill(PLATE, rd)
+            for e in range(2):
+                mm(B(e), A("DG3"), A(Wn, e, QUART, 2), True, False)
+        if rd == 0:
+            to_list("BLk", GM, B(5, 0, 36))
+        fill(SFILL, rd)
 
-    emit(g, T, ops, sent[0])
+    cp(ind(A("LEN"), A("LT")), A("DW"))
+    for c in range(2, 5):
+        q_sums(c)
+        q_out(c)
+        if c == 3:
+            for e in range(2):
+                mm(B(3, 0, 1), A("TRI"), A("CNT", e, e + 1), e == 0, e == 1)
+    to_list("BLh", "GM", B(4, 0, 36))
+    lin("init", B(3, 0, 1), 1.0, -float(HALF))
+    centre = [[9, 11], [-11, -9], [-3, 7], [-7, 3]]
+    for e in range(2):
+        for f in range(4):
+            a = U * centre[f][e] // 2 + K2 - 144 + f % 2
+            mm(B(e), A("ML", 12 - 4 * f, 140 - 4 * f), A("LEN", a, a + PIECE), f == 0, f == 3)
+    to_list("BLd", "DW", B(2, 0, 36), True, False)
+    for e in range(2):
+        d_gather(e)
+        d_round(e)
+    scan(A("OFF", 0, QUART, 2), B(0), A("FL", 0, PIECE), C["init"], Op.min)
+    ts(A("L"), B(4, 0, 36), 287.5)
+    scan(A("OFF", 1, QUART, 2), B(1), A("FL", 0, PIECE), A("OFF", QUART - 2, QUART - 1), Op.min)
+    for e in range(2):
+        tt(P2("GO", e), ind(A("OFF"), L2("L", e)), P2("MK", e), Op.mult)
+    to_list("BLo", "GO", B(2, 0, 36), False, True)
+    d_cut(0)
+    d_cut(1)
+    ts(A("LP"), B(2, 0, 36), float(HALF - 1))
+
+    tt(ind(A("DAT", HALO), A("LP")), A("RD"), A("ZR"), Op.add)
+    for e in range(2):
+        mm(B(6 + e), A("OFFM", p1=32), A("ONES", p1=32), True, False)
+        mm(B(6 + e), A("PEh"), P2("PM", e), False, False)
+    cuts = [(0, FIRST, HALO), (FIRST, QUART, 0)]
+    for e, (c0, c1, lead) in enumerate(cuts):
+        for f in range(4):
+            a = QUART * f + HALO
+            mm(B(e, 0, lead + c1 - c0), shift("EQ", f), A("DAT", a + c0 - lead, a + c1), f == 0, f == 3)
+    slot("carry")
+    for e, (c0, c1, lead) in enumerate(cuts):
+        n = lead + c1 - c0
+        scan(B(2 + e, 0, n), B(e, 0, n), A("FL", 0, n), C["carry"] if e else float(FLOOR), Op.max)
+        if e == 0:
+            cp(C["carry"], B(2, n - 1, n))
+        act(A("TT", c0, c1), B(2 + e, lead, n), 1.0, -127.5)
+    for e, (c0, c1, lead) in enumerate(cuts):
+        tt(A("RR", c0, c1), B(2 + e, lead, lead + c1 - c0), A("TT", c0, c1), Op.subtract)
+    banks = [[4, 5, 0, 1], [2, 3, 4, 5]]
+    for e, (c0, c1, lead) in enumerate(cuts):
+        for f in range(4):
+            b = banks[e][f]
+            mm(B(b, 0, c1 - c0), A("REP", p0=32 * f, p1=32 * f + 32), A("RR", c0, c1, p0=32 * f, p1=32 * f + 32), True, True)
+            (cp if f % 2 else act)(A("XW", QUART * f + c0, QUART * f + c1), B(b, 0, c1 - c0))
+
+    def keep(s, src, queue):
+        if h >= 2 or SENDS[s][2] == h:
+            dma(D(T.y[32 * s:32 * s + 32, :], "y", 4 * s, 4), src(0, 128), queue)
+        else:
+            for f in range(4):
+                dma(D(T.y[32 * s:32 * s + 32, PIECE * f:PIECE * f + PIECE], "y", 4 * s + f), src(32 * f, 32 * f + 32),
+                    "scalar" if f % 2 else "sync")
+
+    cp(P2("OUT", 0), ind(A("XW"), L2("LP", 0)))
+    act(P2("OUT", 1), ind(A("XW"), L2("LP", 1)))
+    first = SENDS[h][1] % 2
+    for e in (first, 1 - first):
+        mm(B(6 + e), A("NEG"), P2("OUT", e), False, True)
+        act(P2("TT", e), B(6 + e), 1.0, -127.5)
+    for e in (first, 1 - first):
+        tt(P2("OUT", 2 + e), B(6 + e), P2("TT", e), Op.subtract)
+    pieces = [P2("OUT", s) for s in SENDS[h]]
+    if h >= 2:
+        mm(B(0), A("NEG"), pieces[2], True, True)
+        pieces[2] = P2("RR", 0)
+        act(pieces[2], B(0), -1.0)
+    for s, src in zip(SENDS[h], pieces):
+        remote([(src, T.YL[h], T.cores[R * z + s], off_engs, "ay%d" % h)])
+    for k, s in enumerate(sorted([s for s in range(R) if s != h], key=lambda s: SENDS[s].index(h))):
+        keep(s, lambda p0, p1: D(T.YL[s, p0:p1, :], "YL", s), "scalar" if k == 2 else "sync")
+        if k == 0:
+            keep(h, lambda p0, p1: A("OUT", PIECE * h, PIECE * h + PIECE, p0=p0, p1=p1), "scalar")
+
+    emit(g, T, ops, sent)
 
 
 def emit(g, T, ops, sent):
     queues = {"v": g.vector, "s": g.scalar, "scalar": g.scalar, "p": g.tensor, "g": g, "sync": g.sync}
     same = {"scalar": "s"}
     csem = {"v": "sv", "s": "ss", "p": "sp", "g": "sg"}
-    writer, readers = {}, {}
+    touched = {}
     for i, o in enumerate(ops):
         deps = set()
         me = same.get(o["q"], o["q"])
-        far = lambda j: ops[j]["kind"] != "c" or o["kind"] != "c" or same.get(ops[j]["q"], ops[j]["q"]) != me
-        for k in o["r"]:
-            if k in writer:
-                deps.add(writer[k])
-            if k[0] == "b" and k[1:].isdigit():
-                deps.update(j for j in readers.get(k, []) if far(j))
-        for k in o["w"]:
-            if k in writer and far(writer[k]):
-                deps.add(writer[k])
-            deps.update(j for j in readers.get(k, []) if far(j))
-        for k in o["r"]:
-            readers.setdefault(k, []).append(i)
-        for k in o["w"]:
-            writer[k] = i
-            readers[k] = []
+        for writes, regs in ((False, o["r"]), (True, o["w"])):
+            for name, p0, p1, c0, c1 in regs:
+                bank = name in SCRATCH and SCRATCH[name][0] == "psum"
+                for j, w, a0, a1, b0, b1 in touched.get(name, []):
+                    far = ops[j]["kind"] != "c" or o["kind"] != "c" or same.get(ops[j]["q"], ops[j]["q"]) != me
+                    meet = p0 < a1 and a0 < p1 and c0 < b1 and b0 < c1
+                    if (far and bank) or (meet and (w or writes) and (far or me != "p")):
+                        deps.add(j)
+        for writes, regs in ((False, o["r"]), (True, o["w"])):
+            for name, p0, p1, c0, c1 in regs:
+                touched.setdefault(name, []).append((i, writes, p0, p1, c0, c1))
         o["deps"] = deps
     seen = {}
     for o in ops:
-        me = same.get(o["q"], o["q"])
+        known = seen.setdefault(same.get(o["q"], o["q"]), {})
         best = {}
         for j in o["deps"]:
             d = ops[j]
             s = csem[d["q"]] if d["kind"] == "c" else d["sem"]
             best[s] = max(best.get(s, -1), j)
         o["waits"] = []
-        for s in sorted(best):
-            if seen.get((me, s), -1) < best[s]:
-                seen[(me, s)] = best[s]
+        for s in sorted(best, key=lambda s: -best[s]):
+            if known.get(s, -1) < best[s]:
+                known[s] = best[s]
+                for s2, j2 in ops[best[s]].get("known", {}).items():
+                    known[s2] = max(known.get(s2, -1), j2)
                 o["waits"].append((s, best[s]))
                 ops[best[s]]["flag"] = True
+        o["known"] = dict(known) if o["kind"] != "x" else {}
     count = {}
     waited = set()
     for o in ops:
@@ -650,7 +711,7 @@ def emit(g, T, ops, sent):
             count[s] = count.get(s, 0) + 1
             ins.then_inc(T.sem[s], 1)
             o["val"] = count[s]
-    g.wait_ge(T.sem.sent, sent)
+    g.wait_ge(T.sem.sent, sent[0])
     for o in ops:
         if o["kind"] in "dx" and o["sem"] not in waited:
             g.sync.wait_ge(T.sem[o["sem"]], o["n"])

from concourse.bass import DstId, RemoteDMATransfer
from concourse.mybir import AluOpType as Op, ActivationFunctionType as Act

N, R, Z, DD = 8, 4, 2304, 6
HALF, QUART, PIECE = Z // 2, Z // 4, Z // 8
LC = Z // 16
HALO = 128
OFFSET = 49152.0
MAGIC = 3221225472.0
FLOOR = 33024
U = 296
K2 = 11 * U // 2 + 144
DUMP = 12 * U
ROUNDS = 7
FIRST = 256


def sb(cols, dtype):
    return ("sbuf", [128, cols], dtype)


SCRATCH = {
    "PS": ("dram", [N * 128, 36], "int32"), "PL": ("dram", [DD, 128, 36], "int32"),
    "XS": ("dram", [N * 128, QUART], "bfloat16"), "XL": ("dram", [N, 128, QUART], "bfloat16"),
    "YL": ("dram", [R, 128, PIECE], "bfloat16"),
    "LAi": sb(LC, "int32"), "LBi": sb(LC, "int32"), "LAh": sb(LC, "float16"), "LBh": sb(LC, "float16"),
    "SaA": sb(228, "float16"), "SaB": sb(228, "float16"), "SbA": sb(228, "float16"), "SbB": sb(228, "float16"),
    "LA": sb(LC, "uint16"), "LB": sb(LC, "uint16"), "Zi": sb(LC, "int32"), "Li": sb(4, "int32"),
    "ZB": sb(LC + 16, "bfloat16"), "XA": sb(Z, "bfloat16"), "XB": sb(Z, "bfloat16"),
    "GA": sb(Z, "bfloat16"), "GB": sb(Z, "bfloat16"), "QW": sb(Z, "float32"),
    "PM": sb(QUART, "float16"), "PEh": sb(128, "float16"), "X": sb(QUART, "float32"), "RD": sb(QUART, "bfloat16"), "ZR": sb(QUART, "bfloat16"),
    "IW": sb(Z + 16, "bfloat16"), "W0": sb(Z, "bfloat16"), "ZW": sb(Z, "bfloat16"),
    "KV": sb(QUART, "bfloat16"), "VAL": sb(QUART, "bfloat16"), "TAB": sb(QUART, "bfloat16"),
    "Wa": sb(QUART, "bfloat16"), "Wb": sb(QUART, "bfloat16"), "GM": sb(QUART, "bfloat16"), "MK": sb(QUART, "bfloat16"),
    "DW": sb(QUART, "bfloat16"), "LEN": sb(DUMP + QUART, "bfloat16"), "OFF": sb(QUART, "float32"), "GO": sb(QUART, "float16"),
    "DAT": sb(Z + HALO, "bfloat16"), "TT": sb(QUART, "bfloat16"), "RR": sb(QUART, "bfloat16"), "XW": sb(Z, "bfloat16"),
    "OUT": sb(HALF, "bfloat16"), "FL": sb(FIRST + HALO, "bfloat16"),
    "L": sb(36, "uint16"), "LI": sb(36, "uint16"), "LT": sb(36, "uint16"), "LP": sb(36, "uint16"), "ZO": sb(36, "uint16"),
    "LTf": sb(36, "float32"), "B1": sb(36, "float32"), "B2": sb(36, "float32"),
    "La": sb(36, "uint16"), "Lb": sb(36, "uint16"), "ZL": sb(LC, "uint16"), "ZLf": sb(LC, "float32"),
    "pi0": sb(1, "int32"), "fi": sb(8, "int32"), "F": sb(8, "float32"), "Cc": sb(100, "float32"),
    "C16": sb(LC, "float32"), "MT": sb(LC, "float32"), "CNT": sb(2, "float32"), "TRI": sb(128, "float32"),
    "Rx": sb(228, "bfloat16"), "H": sb(PIECE, "bfloat16"), "TB": sb(160, "bfloat16"),
    "T8": sb(128, "bfloat16"), "VT": sb(8, "bfloat16"), "VS": sb(12, "bfloat16"), "ZT": sb(16, "bfloat16"), "ML": sb(140, "bfloat16"),
    "ONES": sb(PIECE, "bfloat16"), "OFFM": sb(128, "bfloat16"), "BLo": sb(144, "float16"),
}
for _m in ["SR", "MA", "MB", "WW", "WW0", "DG3", "MM", "NEG", "REP"]:
    SCRATCH[_m] = sb(128, "bfloat16")
for _m in ["EQ", "EA", "EB"]:
    SCRATCH[_m] = sb(228, "bfloat16")
for _m in ["BLh", "BLi", "BLd", "BLk"]:
    SCRATCH[_m] = sb(144, "bfloat16")
for _b in range(8):
    SCRATCH["b%d" % _b] = ("psum", [128, 512], "float32")

NDMA = 44
SEMAPHORES = (["sv", "ss", "sp", "sg", "sent", "hop"] + ["d%d" % i for i in range(NDMA)]
              + ["al%d" % i for i in range(DD)] + ["ax%d" % i for i in range(N)] + ["ay%d" % i for i in range(R)])

CALLS = [[(1, "self", 0), (2, "far", 0)], [(3, "self", 0), (4, "far", 1)], [(5, "self", 0), (6, "far", 2)], [(7, "near", 0)]]
ARRIVAL = [1, 3, 2, 5, 4, 6, 7]
EARLY = 4
SENDS = [[1, 2, 3], [0, 3, 2], [0, 3, 1], [1, 2, 0]]
HOLD = 1


def bits(engs):
    m = 0
    for e in engs:
        m |= 1 << e
    return m


def send_steps(T, topo, q):
    core = T.cores[q]
    side = {"far": [c for c in topo.cores_of(core) if topo.die(c) != topo.die(core)],
            "near": [c for c in topo.cores_of(core) if topo.die(c) == topo.die(core) and c != core]}
    out = []
    for call in CALLS:
        used = []
        for k, how, i in call:
            if how == "self":
                used += topo.engines(core, T.cores[(q + k) % N])
        handed = [c for c in call if c[1] != "self"]
        st = []
        for k, how, i in call:
            d = (q + k) % N
            if how == "self":
                st.append((d, T.cores[d], topo.engines(core, T.cores[d])))
            else:
                c = side[how][i]
                free = [e for e in topo.engines(core, c) if e not in used]
                n = len(free) // len(handed)
                a = handed.index((k, how, i))
                st.append((d, c, free[a * n:a * n + n]))
        out.append(st)
    return out


def rank_program(g, core, T, topo):
    q = T.rank_of(core)
    if q is None:
        for s in range(N):
            for st in send_steps(T, topo, s):
                for d, c, engs in st:
                    if c == core:
                        dst = T.cores[d]
                        rid, pid = topo.addr(dst, core)
                        g.wait_ge(T.sem.hop, len(engs))
                        g.remote_dma(T.XL[s], T.XL[0], T.sem["ax%d" % s], T.sem.sent, pid, rid, topo.mask(core, dst))
                        g.wait_ge(T.sem.sent, len(topo.engines(core, dst)))
        return
    z, h = q // R, q % R
    ops = []
    V = g.vector

    def A(name, c0=0, c1=None, step=1, p0=0, p1=128):
        c1 = SCRATCH[name][1][1] if c1 is None else c1
        ap = T[name][p0:p1, c0:c1] if step == 1 else T[name][p0:p1, c0:c1:step]
        return (ap, [(name, p0, p1, c0, c1)])

    def D(ap, name, i=0, n=1):
        return (ap, [(name, 0, 1, i, i + n)])

    def ind(win, off):
        return (win[0].indirect(off[0]), win[1], off[1])

    def val(a):
        return a[0] if isinstance(a, tuple) else a

    def add(queue, fn, out, ins, kind="c", sem=None, n=0):
        r, w = [], []
        for a in ins:
            if isinstance(a, tuple):
                r += a[1] + (a[2] if len(a) > 2 else [])
        for a in out:
            w += a[1]
            r += a[2] if len(a) > 2 else []
        ops.append({"q": queue, "fn": fn, "r": r, "w": w, "kind": kind, "sem": sem, "n": n})

    ndma = [0]

    def dma(out, in_, queue="sync"):
        eng = g.sync if queue == "sync" else g.scalar
        add(queue, lambda: eng.dma_start(out[0], in_[0]), [out], [in_], "d", "d%d" % ndma[0], 16)
        ndma[0] += 1

    def landed(sem, n, reg):
        add(None, None, [reg], (), "x", sem, n)

    def ts(out, in0, s1, s2=None, o0=Op.add, o1=None):
        if o1 is None:
            add("v", lambda: V.tensor_scalar(out[0], in0[0], val(s1), None, o0), [out], [in0, s1])
        else:
            add("v", lambda: V.tensor_scalar(out[0], in0[0], val(s1), val(s2), o0, o1), [out], [in0, s1, s2])

    def tt(out, in0, in1, o):
        add("v", lambda: V.tensor_tensor(out[0], in0[0], in1[0], o), [out], [in0, in1])

    def cp(out, in_):
        add("v", lambda: V.tensor_copy(out[0], in_[0]), [out], [in_])

    def ms(out, c):
        add("v", lambda: V.memset(out[0], c), [out], ())

    def scan(out, d0, d1, init, o1):
        add("v", lambda: V.tensor_tensor_scan(out[0], d0[0], d1[0], val(init), Op.add, o1), [out], [d0, d1, init])

    def act(out, in_, scale=1.0, bias=0.0, func=Act.Identity, acc=None):
        kw = {} if acc is None else {"accum_out": acc[0]}
        add("s", lambda: g.scalar.activation(out[0], in_[0], func, bias=val(bias), scale=val(scale), **kw),
            [out] + ([] if acc is None else [acc]), [in_, scale, bias])

    def mm(out, lhsT, rhs, start, stop):
        add("p", lambda: g.tensor.matmul(out[0], lhsT[0], rhs[0], start, stop), [out], [lhsT, rhs])

    def iota(out, pattern, base, cm=0, small=True):
        if small:
            add("g", lambda: g.iota(out[0], pattern, base, cm, allow_small_or_imprecise_dtypes=True), [out], ())
        else:
            add("g", lambda: g.iota(out[0], pattern, base, cm), [out], ())

    sent = [0]

    def remote(transfers, after=()):
        tr = []
        for src, dst, c, engs, rsem in transfers:
            rid, pid = topo.addr(c, core)
            tr.append(RemoteDMATransfer(dst_ids=[DstId(rid=rid, pnc=pid)], dma_engine_mask=bits(engs),
                                        remote_sem=T.sem[rsem], src=src[0], dst=dst))
            sent[0] += len(engs)
        add("g", lambda: g.remote_dma_fused(tr, local_sem=T.sem.sent), [], [t[0] for t in transfers] + list(after), "r")

    def B(b, c0=0, c1=PIECE):
        return A("b%d" % b, c0, c1)

    rows = slice(32 * h, 32 * h + 32)
    off_engs = topo.engines(core, T.cores[(q + 1) % N])
    noff = len(off_engs)
    order = [q] + [(q - k) % N for k in ARRIVAL]
    data = [s for s in order if s < DD]
    tiles = {"A": [(q - k) % N for k in range(4)], "B": [(q - k) % N for k in range(4, 8)]}

    def P2(name, e):
        return A(name, PIECE * e, PIECE * e + PIECE)

    def L2(name, e):
        return A(name, 18 * e, 18 * e + 18)

    def shift(name, f, p1=128):
        return A(name, 100 - 32 * f, 228 - 32 * f, p1=p1)

    if q < DD:
        dma(D(T.PS[0:512, :], "PS", 0, 4), D(T.pi[:, 0:LC], "pi"), "sync")
        dma(D(T.PS[512:1024, :], "PS", 4, 4), D(T.pi[:, LC:2 * LC], "pi"), "scalar")
    dma(A("Zi", p1=32), D(T.zero[rows, :], "zero"), "scalar")
    dma(A("Li", 0, 2, p1=32), D(T.lost[rows, :], "lost"), "scalar")

    def where(s):
        return "AB"[(q - s) % N // 4], 32 * ((q - s) % 4)

    def lists_to(s):
        t, p0 = where(s)
        return A("L%si" % t, p0=p0, p1=p0 + 32)

    def load_list(s):
        dma(lists_to(s), D(T.pi[rows, LC * z:LC * z + LC], "pi") if s == q else D(T.PL[s], "PL", s))

    def stage(d):
        dma(D(T.XS[128 * d:128 * d + 128, :], "XS", d),
            D(T.x[32 * (d % R):32 * (d % R) + 32, Z * (d // R):Z * (d // R) + Z], "x"))

    def place(s):
        src = D(T.x[rows, Z * z:Z * z + Z], "x") if s == q else D(T.XL[s], "XL", s)
        t, p0 = where(s)
        dma(A("X" + t, p0=p0, p1=p0 + 32), src)

    for s in range(N):
        if s != q:
            landed("ax%d" % s, noff, D(None, "XL", s))
            if s < DD:
                landed("al%d" % s, 1, D(None, "PL", s))
    for s in range(R):
        if s != h:
            landed("ay%d" % s, noff, D(None, "YL", s))
    steps = send_steps(T, topo, q)
    out_order = [d for st in steps for d, c, engs in st]
    if q < DD:
        load_list(q)
    for d in out_order[:EARLY]:
        stage(d)
    for s in data:
        if s != q:
            load_list(s)
    for d in out_order[EARLY:]:
        stage(d)
    for s in order:
        place(s)
    iota(A("pi0"), [[0, 1]], 0, 1, False)
    iota(A("TB"), [[0, 5], [1, 32]], 0)
    step_e, step_f = [[2, 2], [0, 2]], [[0, 2], [-4, 2]]
    iota(A("VS", 0, 4), step_f, 2)
    iota(A("VS", 4, 8), step_e, -1)
    iota(A("VS", 8, 12), step_f, 2)
    iota(A("VT"), [[0, 4], [1, 2]], 0)
    iota(A("Rx"), [[1, 228]], 0)
    iota(A("C16"), [[16, LC]], 0)
    if q < DD:
        remote([(D(T.PS[128 * d:128 * d + 128, :], "PS", d), T.PL[q], T.cores[d], [off_engs[i]], "al%d" % q)
                for i, d in enumerate([(q + k) % N for k in range(1, N)])])
    iota(A("T8"), [[1, 16], [0, 8]], 0)
    iota(A("ZT", 0, 1), [[0, 1]], 128)
    iota(A("ZT", 1, 16), [[0, 15]], -int(OFFSET))
    for n, st in enumerate(steps):
        remote([(D(T.XS[128 * d:128 * d + 128, :], "XS", d), T.XL[q if c == T.cores[d] else 0], c, engs,
                 "ax%d" % q if c == T.cores[d] else "hop") for d, c, engs in st],
               [lists_to(s) for s in data] if n >= HOLD else [])
    iota(A("ONES"), [[0, PIECE]], 1)
    iota(A("OFFM"), [[0, 128]], int(OFFSET) // 32)
    iota(A("FL"), [[0, FIRST + HALO]], FLOOR)
    iota(A("LEN", 0, DUMP), [[0, DUMP]], 0)
    iota(A("DAT"), [[0, Z + HALO]], 0)

    fields = {"f32": 96, "e16": 16, "p32": 31, "r": 15, "c": 3, "b4": 4}
    C = {}
    ms(A("ZW", 0, QUART), 0.0)
    for i, name in enumerate(fields):
        ts(A("fi", i, i + 1), A("pi0"), fields[name], None, Op.bitwise_and)
        C[name] = A("F", i, i + 1)
    ncol = [0]
    at = {}

    def slot(name, n=1):
        at[name] = ncol[0]
        C[name] = A("Cc", ncol[0], ncol[0] + n)
        ncol[0] += n
        return C[name]

    def col(name, in0, s1, s2, o0, o1=None, n=1):
        ts(slot(name, n), in0, s1, s2, o0, o1)

    def lin(name, in0, scale, bias, n=1):
        act(slot(name, n), in0, scale, bias)

    def el(name, i):
        return A("Cc", at[name] + i, at[name] + i + 1)

    def mat(out, table, code, wgt=None):
        ts(out, table, code, wgt, Op.is_equal, None if wgt is None else Op.mult)

    cp(A("F", 0, len(fields)), A("fi", 0, len(fields)))
    ms(A("ZW", QUART, HALF), 0.0)
    lin("tgt", C["f32"], 1.0 / 32.0, C["e16"])
    lin("cEQ", C["p32"], 1.0, 100.0)
    slot("disk0", 2)
    for n in range(2):
        act(el("disk0", n), C["f32"], -1.0 / 32.0, float(q - 4 * n))
    act(A("VT", p0=32, p1=64), A("VS", 4, 12, p0=32, p1=64))
    act(A("VT", p0=64, p1=96), A("VS", 0, 8, p0=64, p1=96))
    act(A("VT", p0=96), A("VS", 0, 8, p0=96), 0.0, 1.0)
    mat(A("SR"), A("TB", 0, 128), C["tgt"], 1.0 / 16.0)
    col("wrap", C["disk0"], 0.0, float(N), Op.is_lt, Op.mult, n=2)
    mm(B(4, 0, 8), A("SR"), A("VT"), True, True)
    act(A("H", 0, 224), A("Rx", 0, 224), 1.0, -144.0)
    act(A("H", 224, PIECE), A("Rx", 0, 64), 1.0, 80.0)
    tt(slot("disk", 2), C["disk0"], C["wrap"], Op.add)
    col("o", A("Rx", 0, 16), C["r"], None, Op.is_equal, n=16)
    mat(A("EQ"), A("Rx"), C["cEQ"])
    cp(slot("cb", 8), B(4, 0, 8))
    col("flag", el("o", 4), el("o", 5), el("o", 6), Op.add, Op.add)
    lin("k0", C["f32"], 18.0, 144.0)
    ts(A("ZB", 0, LC, p1=32), A("Zi", p1=32), float(Z), None, Op.mult)
    ts(A("MT"), A("C16"), C["r"])
    cp(A("ZB", LC, LC + 2, p1=32), A("Li", 0, 2, p1=32))
    for f in range(4):
        mm(B(5, 0, LC + 2), shift("EQ", f, 32), A("ZB", 0, LC + 2, p1=32), f == 0, f == 3)
    for b in range(8):
        e, f = b // 4, b % 4
        cb = el("cb", 4 * (f // 2) + 2 * e + f % 2)
        blk = A("IW", PIECE * b, PIECE * b + PIECE)
        if b < 5:
            ts(blk, A("H"), el("o", 0), cb, Op.mult, Op.add)
        else:
            act(blk, A("H"), el("o", 0), cb)
    act(A("IW", Z, Z + 16), A("Rx", 0, 16), 0.0, C["flag"])
    tt(A("ZLf"), A("MT"), B(5, 0, LC), Op.max)
    col("qA", B(5, LC, LC + 2), el("disk", 0), None, Op.is_equal, n=2)
    col("qB", B(5, LC, LC + 2), el("disk", 1), None, Op.is_equal, n=2)
    cp(A("ZL"), A("ZLf"))
    lin("kc0", C["k0"], el("o", 15), 0.0)
    lin("rest0", C["flag"], -1.0, 1.0)
    cut = 1440
    act(A("W0", Z - cut, Z), ind(A("IW"), A("ZL", (Z - cut) // 16, LC)))
    for t in "AB":
        for i, s in enumerate(tiles[t]):
            if s >= DD:
                cp(lists_to(s), A("MT", p0=32 * i, p1=32 * i + 32))
    for n, ab in enumerate("ab"):
        for t in "AB":
            mat(A("S" + ab + t), A("Rx"), C["cEQ"], el("q" + t, n))
    cp(A("W0", 0, Z - cut), ind(A("IW"), A("ZL", 0, (Z - cut) // 16)))
    ms(A("ZW", HALF, Z), 0.0)
    for e in range(2):
        for f in range(4):
            mm(B(e), A("EQ", 96 - 32 * f, 224 - 32 * f, p1=32), A("IW", HALF * e + PIECE * f, HALF * e + PIECE * f + PIECE, p1=32),
               f == 0, f == 3)
    for e in range(2):
        for f in range(4):
            mm(B(2, 18 * e, 18 * e + 18), shift("EQ", f, 32), A("ZB", 72 * e + 18 * f, 72 * e + 18 * f + 18, p1=32), f == 0, f == 3)
    lin("kc1", el("o", 15), float(PIECE), C["kc0"])
    lin("rest", el("o", 7), -1.0, C["rest0"])
    for e in range(2):
        act(P2("KV", e), A("H"), el("o", 11), C["kc%d" % e])
    for e in range(2):
        act(P2("TAB", e), B(e), C["flag"], C["rest"])
    col("oc", A("Rx", 0, 4), C["c"], None, Op.is_equal, n=4)
    col("lo8", C["r"], 8.0, None, Op.is_lt)
    lin("s16", C["f32"], 1.0, C["e16"])
    lin("cW0", C["f32"], 0.125, C["e16"])
    lin("xy", el("oc", 1), 1.0, el("oc", 2))
    lin("wh0", el("oc", 0), 2.0, 0.0)
    lin("wk0", C["lo8"], -1.0, 1.0)
    lin("p", C["f32"], 1.0, C["p32"])
    lin("sg", C["b4"], -0.5, 1.0)
    lin("cW", C["c"], 1.0, C["cW0"])
    lin("cBL", C["s16"], 1.0, 15.0)
    lin("cM", C["s16"], 0.125, el("oc", 1))
    lin("wh", C["xy"], 0.5, C["wh0"])
    lin("wk", C["wk0"], el("oc", 3), 0.0)

    for t in "AB":
        ts(A("L%sh" % t), A("L%si" % t), -float(HALF))
    for n, ab in enumerate("ab"):
        for t in "AB":
            for f in range(4):
                mm(B(4 + n, 0, 36), shift("S" + ab + t, f), A("L%sh" % t, 36 * f, 36 * f + 36), t == "A" and f == 0, t == "B" and f == 3)
    ts(A("ZO"), B(2, 0, 36), 1.0, None, Op.min)
    col("cd1", C["f32"], 0.125, 3.0, Op.mult, Op.add)
    ts(A("La"), B(4, 0, 36), float(HALF))
    ts(A("Lb"), B(5, 0, 36), float(HALF))
    cp(P2("VAL", 0), ind(A("W0"), L2("La", 0)))
    act(P2("VAL", 1), ind(A("W0"), L2("La", 1)))
    ts(A("B1"), B(2, 0, 36), -4.0, float(DUMP - K2), Op.mult, Op.add)
    tt(ind(A("ZW"), A("Lb")), A("VAL"), A("KV"), Op.add)
    thirds = [(0, 0, PIECE), (1, 0, 160), (1, 160, PIECE)]
    for n, (e, c0, c1) in enumerate(thirds):
        for f in range(4):
            a = HALF * e + PIECE * f
            mm(B(5 + n, 0, c1 - c0), shift("EQ", f), A("ZW", a + c0, a + c1), f == 0, f == 3)
    mat(A("WW0"), A("TB", 0, 128), C["cW"], C["lo8"])
    mat(A("MM"), A("T8"), C["cM"], C["xy"])
    mat(A("BLh"), A("Rx", 0, 144), C["cBL"], C["wh"])
    mat(A("WW"), A("TB", 0, 128), C["cW"])
    mat(A("DG3"), A("Rx", 0, 128), C["p"], el("oc", 3))
    mat(A("BLk"), A("Rx", 0, 144), C["cBL"], C["wk"])

    def to_list(table, src, out, start=True, stop=True, c0=0, c1=QUART):
        for rho in range(16):
            mm(out, A(table, 15 - rho, 143 - rho), A(src, c0 + rho, c1, 16), start and rho == 0, stop and rho == 15)

    lin("wi0", el("oc", 1), U / 2.0, el("oc", 0))
    lin("noc", el("oc", 0), -1.0, 0.0)
    lin("su", C["e16"], 0.125, -1.0)
    lin("th0", C["e16"], 3.0 / 16.0, 1000.0)
    lin("cP0", C["f32"], 1.0 / 32.0, 0.0)
    lin("wi", el("oc", 2), 5.0 * U / 2.0, C["wi0"])
    lin("th1", C["p32"], C["su"], C["th0"])
    lin("cP", C["p32"], 4.0, C["cP0"])
    lin("th", el("oc", 0), -1000.0, C["th1"])
    act(slot("over5", 2), C["disk"], 1.0, -float(DD - 1), Act.Relu)
    act(slot("over6", 2), C["disk"], 3.0, -3.0 * DD, Act.Relu)
    for n, t in enumerate("AB"):
        lin("gone" + t, el("q" + t, 0), 1.0, el("q" + t, 1))
    for n, t in enumerate("AB"):
        lin("wQ0" + t, el("over5", n), 1.0, C["gone" + t])
        lin("wP0" + t, el("over6", n), -1.0, C["gone" + t])
    for n, t in enumerate("AB"):
        lin("wQ" + t, C["wQ0" + t], 1.0, -1.0)
        lin("wP1" + t, el("over5", n), 2.0, C["wP0" + t])
    for n, t in enumerate("AB"):
        lin("wP" + t, C["wP1" + t], 1.0, -1.0)
    col("wd", C["r"], C["cd1"], None, Op.is_equal)
    tt(A("B2"), A("B1"), A("MT", 0, 36), Op.add)

    def sum_tables():
        for t in "AB":
            cp(A("L" + t), A("L%si" % t))
            mat(A("M" + t), A("TB", 0, 128), C["p32"], C["wQ" + t])
            mat(A("E" + t), A("Rx"), C["cEQ"], C["wP" + t])

    def inverse():
        cp(A("LI"), B(5, 0, 36))

    def order_tables():
        mat(A("BLi"), A("Rx", 0, 144), C["cBL"], C["wi"])
        mat(A("BLo"), A("Rx", 0, 144), C["cBL"], C["noc"])
        mat(A("BLd"), A("Rx", 0, 144), C["cBL"], C["wd"])
        mat(A("ML"), A("TB", 20, 160), C["e16"], C["wd"])
        ts(A("TRI"), A("TB", 0, 128), C["su"], C["th"], Op.mult, Op.is_gt)

    def end_tables():
        mat(A("PEh"), A("Rx", 0, 128), C["cP"])
        mat(A("NEG"), A("Rx", 0, 128), C["cP"], -1.0)
        mat(A("REP"), A("TB", 0, 128), C["p32"])

    turned = [0]

    def turn(fn, n):
        while n:
            t, a = "AB"[turned[0] // Z], turned[0] % Z
            m = min(n, Z - a)
            fn(A("G" + t, a, a + m), ind(A("X" + t), A("L" + t, a // 16, (a + m) // 16)))
            turned[0] += m
            n -= m

    QCH = [(0, 512, 7), (512, 960, 5), (960, 1408, 6), (1408, 1856, 7), (1856, Z, 5)]
    sums = []
    for t in "AB":
        for e in range(2):
            for f in range(4):
                a = HALF * e + PIECE * f
                sums.append((B(5 + e), shift("E" + t, f), A("X" + t, a, a + PIECE), t == "A" and f == 0, t == "B" and f == 3))

    def p_sums(n):
        for i in range(n):
            mm(*sums.pop(0))

    def p_out(e):
        cp(P2("PM", e), B(5 + e))

    def q_sums(c):
        a, b, bank = QCH[c]
        for t in "AB":
            mm(B(bank, 0, b - a), A("M" + t), A("G" + t, a, b), t == "A", t == "B")

    def q_out(c, queue="s"):
        a, b, bank = QCH[c]
        if queue == "s":
            act(A("QW", a, b), B(bank, 0, b - a), 1.0, 128.0)
        else:
            ts(A("QW", a, b), B(bank, 0, b - a), 128.0)

    def d_gather(e):
        tt(P2("X", e), ind(A("QW"), L2("LI", e)), P2("PM", e), Op.subtract)

    def d_round(e):
        act(B(5 + e), P2("X", e), 1.0, MAGIC)
        act(B(5 + e), B(5 + e), 1.0, -MAGIC)

    def d_cut(e):
        tt(P2("RD", e), B(5 + e), P2("X", e), Op.subtract)

    VFILL = {0: [(sum_tables,)], 1: [(inverse,), (order_tables,)], 2: [(turn, cp, 512)], 3: [(turn, cp, 512)],
             4: [(turn, cp, 512)], 5: [(turn, cp, 512)], 6: [(turn, cp, 192), (p_out, 0), (p_out, 1)],
             7: [(q_out, 0, "v"), (end_tables,)]}
    SFILL = {0: [(act, A("ZR"), ind(A("ZT"), A("ZO")))], 1: [(turn, act, 448)], 2: [(turn, act, 416)], 3: [(turn, act, 416)], 4: [(turn, act, 416)], 5: [(turn, act, 416)],
             6: [(turn, act, 256)]}
    PLATE = {2: [(p_sums, 3)], 3: [(p_sums, 3)], 4: [(p_sums, 3)], 5: [(p_sums, 3)], 6: [(q_sums, 0)]}
    PEARLY = {3: [(p_sums, 1)], 4: [(p_sums, 1)], 5: [(p_sums, 1)], 6: [(p_sums, 1)],
              7: [(q_sums, 1), (q_out, 1)]}

    def fill(table, rd):
        for job in table.get(rd, []):
            job[0](*job[1:])

    for rd in range(ROUNDS + 1):
        W, Wn = "W" + "ba"[rd % 2], "W" + "ab"[rd % 2]
        GM = "GM" if rd else "VAL"
        last = rd == ROUNDS

        def gather(e):
            if rd == 0:
                for n, (half, c0, c1) in enumerate(thirds):
                    if half == e:
                        tt(A(GM, PIECE * e + c0, PIECE * e + c1), B(5 + n, 0, c1 - c0), A("TAB", PIECE * e + c0, PIECE * e + c1), Op.mult)
            else:
                tt(P2(GM, e), ind(A(W), L2("L", e)), P2("MK", e), Op.mult)

        def window(e):
            mm(B(e), A("WW" if rd else "WW0"), P2(GM, e), rd == 0, True)
            if last:
                act(P2("DW", e), B(e), 1.0, 1.0)
            else:
                act(A(Wn, e, QUART, 2), B(e))

        def mask(e):
            mm(B(2 + e), A("MM"), P2(GM, e), True, True)
            act(P2("MK", e), B(2 + e), C["sg"], -1.0, Act.Relu, A("CNT", e, e + 1) if last else None)

        gather(0)
        gather(1)
        window(0)
        mask(0)
        fill(PEARLY, rd)
        fill(VFILL, rd)
        if last:
            to_list("BLi", GM, B(4, 64, 100))
            window(1)
            tt(A("LTf"), B(4, 64, 100), A("B2"), Op.max)
            ts(A("LT"), A("LTf"), float(K2))
            mask(1)
        else:
            window(1)
            to_list("BLh", GM, B(4, 0, 36))
            ts(A("L"), B(4, 0, 36), 287.5)
            mask(1)
            fill(PLATE, rd)
            for e in range(2):
                mm(B(e), A("DG3"), A(Wn, e, QUART, 2), True, False)
        if rd == 0:
            to_list("BLk", GM, B(5, 0, 36))
        fill(SFILL, rd)

    cp(ind(A("LEN"), A("LT")), A("DW"))
    for c in range(2, 5):
        q_sums(c)
        q_out(c)
        if c == 3:
            for e in range(2):
                mm(B(3, 0, 1), A("TRI"), A("CNT", e, e + 1), e == 0, e == 1)
    to_list("BLh", "GM", B(4, 0, 36))
    lin("init", B(3, 0, 1), 1.0, -float(HALF))
    centre = [[9, 11], [-11, -9], [-3, 7], [-7, 3]]
    for e in range(2):
        for f in range(4):
            a = U * centre[f][e] // 2 + K2 - 144 + f % 2
            mm(B(e), A("ML", 12 - 4 * f, 140 - 4 * f), A("LEN", a, a + PIECE), f == 0, f == 3)
    to_list("BLd", "DW", B(2, 0, 36), True, False)
    for e in range(2):
        d_gather(e)
        d_round(e)
    scan(A("OFF", 0, QUART, 2), B(0), A("FL", 0, PIECE), C["init"], Op.min)
    ts(A("L"), B(4, 0, 36), 287.5)
    scan(A("OFF", 1, QUART, 2), B(1), A("FL", 0, PIECE), A("OFF", QUART - 2, QUART - 1), Op.min)
    for e in range(2):
        tt(P2("GO", e), ind(A("OFF"), L2("L", e)), P2("MK", e), Op.mult)
    to_list("BLo", "GO", B(2, 0, 36), False, True)
    d_cut(0)
    d_cut(1)
    ts(A("LP"), B(2, 0, 36), float(HALF - 1))

    tt(ind(A("DAT", HALO), A("LP")), A("RD"), A("ZR"), Op.add)
    for e in range(2):
        mm(B(6 + e), A("OFFM", p1=32), A("ONES", p1=32), True, False)
        mm(B(6 + e), A("PEh"), P2("PM", e), False, False)
    cuts = [(0, FIRST, HALO), (FIRST, QUART, 0)]
    for e, (c0, c1, lead) in enumerate(cuts):
        for f in range(4):
            a = QUART * f + HALO
            mm(B(e, 0, lead + c1 - c0), shift("EQ", f), A("DAT", a + c0 - lead, a + c1), f == 0, f == 3)
    slot("carry")
    for e, (c0, c1, lead) in enumerate(cuts):
        n = lead + c1 - c0
        scan(B(2 + e, 0, n), B(e, 0, n), A("FL", 0, n), C["carry"] if e else float(FLOOR), Op.max)
        if e == 0:
            cp(C["carry"], B(2, n - 1, n))
        act(A("TT", c0, c1), B(2 + e, lead, n), 1.0, -127.5)
    for e, (c0, c1, lead) in enumerate(cuts):
        tt(A("RR", c0, c1), B(2 + e, lead, lead + c1 - c0), A("TT", c0, c1), Op.subtract)
    banks = [[4, 5, 0, 1], [2, 3, 4, 5]]
    for e, (c0, c1, lead) in enumerate(cuts):
        for f in range(4):
            b = banks[e][f]
            mm(B(b, 0, c1 - c0), A("REP", p0=32 * f, p1=32 * f + 32), A("RR", c0, c1, p0=32 * f, p1=32 * f + 32), True, True)
            (cp if f % 2 else act)(A("XW", QUART * f + c0, QUART * f + c1), B(b, 0, c1 - c0))

    def keep(s, src, queue):
        if h >= 2 or SENDS[s][2] == h:
            dma(D(T.y[32 * s:32 * s + 32, :], "y", 4 * s, 4), src(0, 128), queue)
        else:
            for f in range(4):
                dma(D(T.y[32 * s:32 * s + 32, PIECE * f:PIECE * f + PIECE], "y", 4 * s + f), src(32 * f, 32 * f + 32),
                    "scalar" if f % 2 else "sync")

    cp(P2("OUT", 0), ind(A("XW"), L2("LP", 0)))
    act(P2("OUT", 1), ind(A("XW"), L2("LP", 1)))
    first = SENDS[h][1] % 2
    for e in (first, 1 - first):
        mm(B(6 + e), A("NEG"), P2("OUT", e), False, True)
        act(P2("TT", e), B(6 + e), 1.0, -127.5)
    for e in (first, 1 - first):
        tt(P2("OUT", 2 + e), B(6 + e), P2("TT", e), Op.subtract)
    pieces = [P2("OUT", s) for s in SENDS[h]]
    if h >= 2:
        mm(B(0), A("NEG"), pieces[2], True, True)
        pieces[2] = P2("RR", 0)
        act(pieces[2], B(0), -1.0)
    for s, src in zip(SENDS[h], pieces):
        remote([(src, T.YL[h], T.cores[R * z + s], off_engs, "ay%d" % h)])
    for k, s in enumerate(sorted([s for s in range(R) if s != h], key=lambda s: SENDS[s].index(h))):
        keep(s, lambda p0, p1: D(T.YL[s, p0:p1, :], "YL", s), "scalar" if k == 2 else "sync")
        if k == 0:
            keep(h, lambda p0, p1: A("OUT", PIECE * h, PIECE * h + PIECE, p0=p0, p1=p1), "scalar")

    emit(g, T, ops, sent)


def emit(g, T, ops, sent):
    queues = {"v": g.vector, "s": g.scalar, "scalar": g.scalar, "p": g.tensor, "g": g, "sync": g.sync}
    same = {"scalar": "s"}
    csem = {"v": "sv", "s": "ss", "p": "sp", "g": "sg"}
    touched = {}
    for i, o in enumerate(ops):
        deps = set()
        me = same.get(o["q"], o["q"])
        for writes, regs in ((False, o["r"]), (True, o["w"])):
            for name, p0, p1, c0, c1 in regs:
                bank = name in SCRATCH and SCRATCH[name][0] == "psum"
                for j, w, a0, a1, b0, b1 in touched.get(name, []):
                    far = ops[j]["kind"] != "c" or o["kind"] != "c" or same.get(ops[j]["q"], ops[j]["q"]) != me
                    meet = p0 < a1 and a0 < p1 and c0 < b1 and b0 < c1
                    if (far and bank) or (meet and (w or writes) and (far or me != "p")):
                        deps.add(j)
        for writes, regs in ((False, o["r"]), (True, o["w"])):
            for name, p0, p1, c0, c1 in regs:
                touched.setdefault(name, []).append((i, writes, p0, p1, c0, c1))
        o["deps"] = deps
    seen = {}
    for o in ops:
        known = seen.setdefault(same.get(o["q"], o["q"]), {})
        best = {}
        for j in o["deps"]:
            d = ops[j]
            s = csem[d["q"]] if d["kind"] == "c" else d["sem"]
            best[s] = max(best.get(s, -1), j)
        o["waits"] = []
        for s in sorted(best, key=lambda s: -best[s]):
            if known.get(s, -1) < best[s]:
                known[s] = best[s]
                for s2, j2 in ops[best[s]].get("known", {}).items():
                    known[s2] = max(known.get(s2, -1), j2)
                o["waits"].append((s, best[s]))
                ops[best[s]]["flag"] = True
        o["known"] = dict(known) if o["kind"] != "x" else {}
    count = {}
    waited = set()
    for o in ops:
        if o["kind"] == "x":
            o["val"] = o["n"]
            continue
        eng = queues[o["q"]]
        for s, j in o["waits"]:
            eng.wait_ge(T.sem[s], ops[j]["val"])
            waited.add(s)
        ins = o["fn"]()
        if o["kind"] == "d":
            ins.then_inc(T.sem[o["sem"]], 16)
            o["val"] = 16
        elif o["kind"] == "c" and o.get("flag"):
            s = csem[o["q"]]
            count[s] = count.get(s, 0) + 1
            ins.then_inc(T.sem[s], 1)
            o["val"] = count[s]
    g.wait_ge(T.sem.sent, sent[0])
    for o in ops:
        if o["kind"] in "dx" and o["sem"] not in waited:
            g.sync.wait_ge(T.sem[o["sem"]], o["n"])
